import numpy as np, ml_dtypes
CORES = [3,11,19,27,35,43,51,59]
N = 8
import mx_ref
BF = ml_dtypes.bfloat16
def entries(a):
    return np.ascontiguousarray(a.T).reshape(-1)
def table(e):
    return np.ascontiguousarray(np.reshape(e, (-1, 16)).T).astype(np.int32)
def cols(t, e):
    v = np.concatenate([t.reshape(128, -1, 4), np.zeros((128, 1, 4), BF)], axis=1)
    return np.ascontiguousarray(v[:, e]).reshape(128, -1)
def cut(t, i, w=512):
    return t[:, w * i:w * i + w]
def f(rng, *shape):
    return mx_ref.flush((rng.standard_normal(shape, dtype=np.float32) * np.exp2(rng.integers(-2, 3, shape[:-1] + (1,)))).astype(BF))
def wide(rng, *shape, cols=0):
    v = rng.standard_normal(shape, dtype=np.float32) * np.exp2(rng.integers(-12, 13, shape)).astype(np.float32)
    if cols: v *= np.repeat(np.exp2(rng.integers(-cols, cols + 1, shape[:-2] + (1, shape[-1] // 4))) * (rng.random(shape[:-2] + (1, shape[-1] // 4)) > 0.0625), 4, axis=-1).astype(np.float32)
    return mx_ref.flush(v.astype(BF))
T, CAPP, F = 128, 96, 8
def inverse(e):
    o = np.full(F * T, -1)
    k = np.flatnonzero(e >= 0); k = k[np.argsort(e[k], kind="stable")]; v = e[k]
    at = np.arange(len(k)) - np.searchsorted(v, v); keep = at < F
    o[(F * v + at)[keep]] = k[keep]
    return o
def counts(rng, most=CAPP):
    n = np.zeros((N, N), int)
    for r in range(N):
        a = rng.integers(T // N, 4 * T // N + 1, N)
        n[:, r] = a + np.bincount(rng.permutation(np.repeat(np.arange(N), most - a))[:4 * T - a.sum()], minlength=N)
    return n
def senders(rng, n):
    return np.stack([rng.permutation(np.repeat(np.arange(N), n[:, r])) for r in range(N)])
def lists(rng, A, node=None, top=None, popular=False, big=None):
    sn = np.full((N, N * CAPP), -1); nb = np.zeros((N, 4 * T), int)
    for s in range(N):
        d, e = np.nonzero(A == s); free = rng.permutation(T)
        if node is not None: v = node[d, e]
        elif top is not None:
            t = top[d, e]; h = (t.sum() + F - 1) // F; v = np.zeros(len(d), int); big.append(free[:h])
            v[t] = rng.permutation(np.repeat(free[:h], F))[:t.sum()]
            v[~t] = rng.permutation(np.repeat(free[h:], F))[:(~t).sum()]
        else:
            h = len(d) // 16 if popular else 0
            v = rng.permutation(np.concatenate([np.repeat(free[:h], F), rng.permutation(np.repeat(free[h:], F))[:len(d) - F * h]]))
        for q in range(N):
            k = np.flatnonzero(d == q); c = rng.permutation(CAPP)[:len(k)]
            sn[s, q * CAPP + c] = v[k]; nb[q, e[k]] = s * CAPP + c
    return {"sn": np.stack([table(a) for a in sn]), "nb": np.stack([table(a) for a in nb]), "il": np.stack([table(inverse(a)) for a in sn])}
def setup_inputs(rng):
    return {"x": f(rng, N, 128, 4 * T), "gr": f(rng, N, 128, 4 * T), "w": np.repeat(f(rng, 1, 128, 2048), N, axis=0), "w2": np.repeat(f(rng, 1, 128, 2048), N, axis=0), **lists(rng, senders(rng, counts(rng)))}
def setup_inputs_ties(rng):
    d = setup_inputs(rng); own = d["x"].reshape(N, 128, T, 4)
    d["x"] = np.ascontiguousarray(np.where(rng.random((N, 1, T, 1)) < 0.7, own[:1], own)).reshape(N, 128, 4 * T)
    n = counts(rng, min(CAPP, T)); A = np.zeros((N, 4 * T), int); node = np.zeros((N, 4 * T), int)
    e = np.arange(4 * T); j = e % T; k = (e // T + j) % 4
    for r in range(N):
        o = rng.permutation(N); to = 4 * rng.permutation(T)[j] + k
        A[r, to] = np.repeat(o, n[o, r]); node[r, to] = rng.permutation(T)[j]
    return {**d, **lists(rng, A, node=node)}
def setup_inputs_oneside(rng):
    d = setup_inputs(rng); top = np.zeros((N, 4 * T), bool); big = []
    for r in range(N): top[r, 4 * rng.permutation(T)[:T // 2] + 3] = True
    d.update(lists(rng, senders(rng, counts(rng)), top=top, big=big))
    v = np.abs(d["x"].astype(np.float32)).reshape(N, 128, T, 4)
    for s in range(N): v[s][:, big[s]] *= 64
    d["x"] = v.reshape(N, 128, 4 * T).astype(BF); d["w"] = np.abs(d["w"].astype(np.float32)).astype(BF)
    return d
def setup_inputs_popular(rng):
    return {**setup_inputs(rng), **lists(rng, senders(rng, counts(rng)), popular=True)}
def setup_inputs_full(rng):
    n = np.zeros((N, N), int); o = rng.permutation(N); at = rng.permutation(N)
    m = 4 * T // CAPP; rest = 4 * T - m * CAPP
    for r in range(N):
        for j in range(m): n[o[(at[r] + j) % N], r] = CAPP
        if rest: n[o[(at[r] + m) % N], r] = rest
    return {**setup_inputs(rng), **lists(rng, senders(rng, n))}
def setup_inputs_spread(rng):
    d = setup_inputs(rng); d["x"] = wide(rng, N, 128, 4 * T, cols=8); return d
def check_inputs(d):
    b = []
    for t in ("w", "w2"):
        if (d[t] != d[t][:1]).any(): b.append(t)
    e = np.stack([entries(a) for a in d["sn"]])
    if e.min() < -1 or e.max() >= T: b.append("sn")
    e = np.clip(e, -1, T - 1)
    for r in range(N):
        if np.bincount(e[r][e[r] >= 0], minlength=T).max() > F: b.append("sn")
        if not np.array_equal(np.sort(entries(d["nb"][r])), np.flatnonzero(e[:, r * CAPP:(r + 1) * CAPP].reshape(-1) >= 0)): b.append("nb")
        if not np.array_equal(entries(d["il"][r]), inverse(e[r])): b.append("il")
    return b
def four(v):
    return [mx_ref.quantize(np.ascontiguousarray(cut(v, b))) for b in range(4)]
def reference(x, gr, w, w2, sn, nb, il):
    G = []
    for r in range(N):
        arrived = mx_ref.quantize(np.concatenate([cols(x[s], entries(sn[s])[r * CAPP:(r + 1) * CAPP]) for s in range(N)], axis=1))
        e = entries(nb[r])
        z = [mx_ref.matmul(W, arrived)[:, e].reshape(128, T, 4) + np.float32(0.0) for W in four(w[r])]
        win = np.stack([v.argmax(axis=2) for v in z], axis=2)
        g = gr[r].reshape(128, T, 4); back = np.zeros((128, N * CAPP, 4), BF)
        for k in range(4): back[:, e[k::4]] = np.where(win == k, g, np.zeros_like(g))
        G.append(back)
    y = np.zeros((N, 128, 4 * T), np.float32)
    for s in range(N):
        q = mx_ref.quantize(np.concatenate([G[r][:, s * CAPP:(s + 1) * CAPP].reshape(128, -1) for r in range(N)], axis=1))
        e = entries(il[s])
        for b, V in enumerate(four(w2[s])):
            u = mx_ref.matmul(V, q); t = np.zeros((128, T), np.float32)
            for i in range(F):
                k = e[i::F]; has = k >= 0
                t[:, has] += u[:, k[has]]
            y[s][:, T * b:T * b + T] = t
    return {"y": y}

@@ -1,0 +1,374 @@
+import numpy as np
+from concourse.bass import DstId, RemoteDMATransfer
+from concourse.mybir import dt, AluOpType, ActivationFunctionType
+
+N, NT, CAP, HB = 8, 128, 96, 384
+UW = 776
+CODES = "float8_e4m3fn_x4"
+
+SCRATCH = {
+    "xb": ("sbuf", [128, 528], "bfloat16"),
+    "snw": ("sbuf", [128, 48], "int32"),
+    "snof": ("sbuf", [128, 192], "uint16"),
+    "xt": ("sbuf", [128, 3072], "bfloat16"),
+    "fc": ("sbuf", [128, 768], CODES), "fs": ("sbuf", [128, 768], "uint8"),
+    "rc": ("sbuf", [128, 768], CODES), "rs": ("sbuf", [128, 768], "uint8"),
+    "wb": ("sbuf", [128, 2048], "bfloat16"),
+    "wq": ("sbuf", [128, 512], CODES), "ws": ("sbuf", [128, 512], "uint8"),
+    "vb": ("sbuf", [128, 2048], "bfloat16"),
+    "vq": ("sbuf", [128, 512], CODES), "vs": ("sbuf", [128, 512], "uint8"),
+    "zp": ("psum", [128, 4096], "float32"),
+    "zb": ("sbuf", [128, 3072], "float32"),
+    "nbd": ("dram", [16, 32], "int32"),
+    "nbw": ("sbuf", [128, 32], "int32"),
+    "zof": ("sbuf", [128, 64], "uint16"),
+    "pa": ("sbuf", [128, 32], "int32"), "pb": ("sbuf", [128, 32], "int32"),
+    "pc": ("sbuf", [128, 32], "int32"), "pd": ("sbuf", [128, 32], "int32"),
+    "pof": ("sbuf", [128, 32], "uint16"),
+    "ivv": ("sbuf", [128, 512], "int32"),
+    "inv": ("sbuf", [128, 768], "int32"),
+    "invw": ("sbuf", [128, 48], "int32"),
+    "ivo": ("sbuf", [128, 48], "uint16"),
+    "pi": ("sbuf", [128, 1], "int32"),
+    "k15": ("sbuf", [128, 1], "int32"), "k3": ("sbuf", [128, 1], "int32"), "k12": ("sbuf", [128, 1], "int32"),
+    "f8": ("sbuf", [128, 1], "float32"), "f12": ("sbuf", [128, 1], "float32"), "fgr": ("sbuf", [128, 1], "float32"),
+    "ilpat": ("sbuf", [128, 64], "int32"), "grpat": ("sbuf", [128, 32], "int32"),
+    "grb": ("sbuf", [128, 512], "bfloat16"), "gro": ("sbuf", [128, 32], "uint16"),
+    "z0": ("sbuf", [128, 512], "float32"), "m1": ("sbuf", [128, 512], "float32"), "m2": ("sbuf", [128, 512], "float32"),
+    "d0": ("sbuf", [128, 2048], "bfloat16"), "d1": ("sbuf", [128, 2048], "bfloat16"),
+    "rr": ("sbuf", [128, 4096], "bfloat16"), "e0": ("sbuf", [128, 4096], "bfloat16"),
+    "gg": ("sbuf", [128, 4096], "bfloat16"),
+    "h": ("sbuf", [128, 3072], "bfloat16"),
+    "bc": ("sbuf", [128, 768], CODES), "bs": ("sbuf", [128, 768], "uint8"),
+    "qc": ("sbuf", [128, 768], CODES), "qs": ("sbuf", [128, 768], "uint8"),
+    "ub": ("sbuf", [128, 4 * UW], "float32"),
+    "ilf": ("sbuf", [128, 1024], "int32"), "ilo": ("sbuf", [128, 64], "uint16"),
+    "ilp": ("sbuf", [128, 1024], "int32"), "ilw": ("sbuf", [128, 64], "int32"),
+    "ila": ("sbuf", [128, 64], "int32"), "ilb": ("sbuf", [128, 64], "int32"),
+    "ilq": ("sbuf", [128, 64], "uint16"),
+    "a0": ("sbuf", [128, 1024], "float32"), "a1": ("sbuf", [128, 1024], "float32"),
+    "a2": ("sbuf", [128, 1024], "float32"), "a3": ("sbuf", [128, 1024], "float32"),
+    "yb": ("sbuf", [128, 512], "float32"),
+}
+SEMAPHORES = ["cv", "cs", "ct", "cp", "d_x", "d_sn", "d_w", "d_v", "d_gr", "d_nd", "d_nb", "d_il", "d_iv", "d_ih",
+              "d_of", "d_ob", "d_y", "fa0", "fa1", "ba0", "ba1", "ls"]
+
+
+def half_sends(s, half, cores, topo):
+    ds = [d for d in range(4 * half, 4 * half + 4) if d != s]
+    if len(ds) == 4:
+        cut_c = cut_p = [(0, 2), (2, 4), (4, 6), (6, 8)]
+    else:
+        cut_c, cut_p = [(0, 4), (4, 6), (6, 8)], [(0, 2), (2, 4), (4, 8)]
+    out = []
+    for d, (a, b), (u, v) in zip(ds, cut_c, cut_p):
+        e = topo.engines(cores[s], cores[d])
+        out.append((d, e[a:b], e[u:v]))
+    return out
+
+
+def arrivals(r, half, cores, topo):
+    n = 0
+    for s in range(4 * half, 4 * half + 4):
+        if s != r:
+            for d, ec, ep in half_sends(s, r // 4, cores, topo):
+                if d == r:
+                    n += len(ec) + len(ep)
+    return n
+
+
+def rank_program(g, core, T, topo):
+    r = T.rank_of(core)
+    if r is None:
+        return
+    A, COPY, IDENT = AluOpType, ActivationFunctionType.Copy, ActivationFunctionType.Identity
+    cores = list(T.cores)
+    hr, ho = r // 4, 1 - r // 4
+    V, S, P, Y = g.vector, g.scalar, g.tensor, g.sync
+    qn = {"V": V, "S": S, "P": P, "Y": Y, "G": g}
+    cnt, seen = {}, {}
+
+    def done(ins, sem, n=1):
+        ins.then_inc(T.sem[sem], n)
+        cnt[sem] = cnt.get(sem, 0) + n
+        return (sem, cnt[sem])
+
+    def need(q, *marks):
+        best = {}
+        for m in marks:
+            if m is not None:
+                best[m[0]] = max(best.get(m[0], 0), m[1])
+        for sem, val in best.items():
+            if seen.get((q, sem), 0) < val:
+                qn[q].wait_ge(T.sem[sem], val)
+                seen[(q, sem)] = val
+
+    def dv(ins): return done(ins, "cv")
+    def ds(ins): return done(ins, "cs")
+    def dp(ins): return done(ins, "ct")
+    def dg(ins): return done(ins, "cp")
+
+    x_in = done(S.dma_start(T.xb[:, 16:528], T.x[:, :]), "d_x", 16)
+    for k in range(5):
+        done(Y.dma_start(T.snw[16 * k:16 * k + 16, :], T.sn[:, :]), "d_sn", 16)
+    for k in range(5, 8):
+        sn_in = done(S.dma_start(T.snw[16 * k:16 * k + 16, :], T.sn[:, :]), "d_sn", 16)
+    for k in range(4):
+        nd_in = done(Y.dma_start(T.nbd[:, 8 * k:8 * k + 8], T.nb[k:16:4, :]), "d_nd", 16)
+    w_in = done(Y.dma_start(T.wb[:, :], T.w[:, :]), "d_w", 16)
+    gr_in = done(S.dma_start(T.grb[:, :], T.gr[:, :]), "d_gr", 16)
+    need("Y", nd_in)
+    for k in range(8):
+        nb_in = done(Y.dma_start(T.nbw[16 * k:16 * k + 16, :], T.nbd[:, :]), "d_nb", 16)
+    v_in = done(Y.dma_start(T.vb[:, :], T.w2[:, :]), "d_v", 16)
+
+    m_pi = dg(g.iota(T.pi[:, :], [[0, 1]], 0, 1))
+    m_grp = dg(g.iota(T.grpat[:, :], [[1, 4], [16, 8]], 0, 0))
+    m_ivv = dg(g.iota(T.ivv[:, :], [[-2, 4], [8, 128]], 7, 0))
+    m_ilp = dg(g.iota(T.ilpat[:, :], [[1, 8], [512, 2], [128, 4]], 0, 0))
+
+    m_pad = dv(V.memset(T.xb[:, 0:16], 0.0))
+    need("V", m_pi)
+    k15 = dv(V.tensor_scalar(T.k15[:, :], T.pi[:, :], 15, None, A.bitwise_and))
+    k3 = dv(V.tensor_scalar(T.k3[:, :], T.pi[:, :], 3, None, A.bitwise_and))
+    k12 = dv(V.tensor_scalar(T.k12[:, :], T.pi[:, :], 12, None, A.bitwise_and))
+    m_ilf = dv(V.memset(T.ilf[:, :], 0))
+    m_inv = dv(V.memset(T.inv[:, :], 0))
+    need("V", k12)
+    m_f8 = dv(V.tensor_scalar(T.f8[:, :], T.k15[:, :], 8, None, A.mult))
+    m_f12 = dv(V.tensor_copy(T.f12[:, :], T.k12[:, :]))
+    need("Y", m_ilf)
+    il_in = done(Y.dma_start(T.ilf[0:1, :], T.il[:, :]), "d_il", 16)
+
+    need("V", sn_in)
+    snof = []
+    for t in range(4):
+        snof.append(dv(V.tensor_scalar(T.snof[:, 48 * t:48 * t + 48], T.snw[:, :], 4, 16 + t, A.mult, A.add)))
+
+    def sends(codes, planes, lc, lp, half, sem):
+        for own, land, w in ((codes, lc, 0), (planes, lp, 1)):
+            tr = []
+            for d, ec, ep in half_sends(r, half, cores, topo):
+                rid, pid, _ = topo.addr(cores[d])
+                mask = sum(1 << e for e in (ep if w else ec))
+                src, dst = own[:, CAP * d:CAP * d + CAP], land[:, CAP * r:CAP * r + CAP]
+                if not w:
+                    src, dst = src.bitcast(dt.uint8), dst.bitcast(dt.uint8)
+                tr.append(RemoteDMATransfer(dst_ids=[DstId(rid=rid, pnc=pid)], dma_engine_mask=mask,
+                                            remote_sem=T.sem[sem], srcs=[src], dsts=[dst]))
+                cnt["ls"] = cnt.get("ls", 0) + len(ep if w else ec)
+            g.remote_dma_fused(tr, local_sem=T.sem["ls"])
+
+    def own_block(codes, planes, lc, lp, sem):
+        a, b = CAP * r, CAP * r + CAP
+        done(Y.dma_start(lc[:, a:b].bitcast(dt.uint8), codes[:, a:b].bitcast(dt.uint8)), sem, 16)
+        return done(Y.dma_start(lp[:, a:b], planes[:, a:b]), sem, 16)
+
+    for half in (ho, hr):
+        win = T.xb[:, 0:528]
+        marks = []
+        for q, t in (("S", 0), ("V", 2), ("S", 1), ("V", 3)):
+            need(q, x_in, m_pad, snof[t])
+            out = T.xt[:, 4 * HB * half + t:4 * HB * (half + 1):4]
+            src = win.indirect(T.snof[:, 48 * t + 24 * half:48 * t + 24 * half + 24])
+            marks.append(ds(S.activation(out, src, COPY)) if q == "S" else dv(V.tensor_copy(out, src)))
+        need("V", *marks)
+        f_q = dv(V.quantize_mx(T.fc[:, HB * half:HB * half + HB], T.fs[:, HB * half:HB * half + HB],
+                               T.xt[:, 4 * HB * half:4 * HB * half + 4 * HB]))
+        need("G", f_q)
+        sends(T.fc, T.fs, T.rc, T.rs, half, "fa%d" % hr)
+    need("Y", f_q)
+    own_f = own_block(T.fc, T.fs, T.rc, T.rs, "d_of")
+
+    m_rr = dg(g.iota(T.rr[:, 1:4096:2], [[0, 2048]], 0, 0, allow_small_or_imprecise_dtypes=True))
+    m_ee = dg(g.iota(T.e0[:, 0:4096:2], [[0, 2048]], 0, 0, allow_small_or_imprecise_dtypes=True))
+    m_e1 = dg(g.iota(T.e0[:, 7:4096:8], [[0, 512]], 1, 0, allow_small_or_imprecise_dtypes=True))
+
+    m_d1 = dv(V.memset(T.d1[:, :], 0.0))
+    need("V", m_f12, k3)
+    m_fgr = dv(V.tensor_scalar(T.fgr[:, :], T.k3[:, :], 128, T.f12[:, :], A.mult, A.add))
+    need("V", w_in)
+    w_q = dv(V.quantize_mx(T.wq[:, 0:512], T.ws[:, 0:512], T.wb[:, 0:2048]))
+    need("V", m_fgr, m_grp)
+    m_gro = dv(V.tensor_scalar(T.gro[:, :], T.grpat[:, :], T.fgr[:, :], None, A.add))
+    need("S", m_d1, m_gro, gr_in)
+    d1_ok = ds(S.activation(T.d1[:, 0:2048:4], T.grb[:, 0:512].indirect(T.gro[:, 0:32]), COPY))
+
+    need("V", nb_in)
+    p_a = dv(V.tensor_scalar(T.pa[:, :], T.nbw[:, :], 15, None, A.bitwise_and))
+    p_b = dv(V.tensor_scalar(T.pb[:, :], T.nbw[:, :], 4, None, A.arith_shift_right))
+    need("V", p_a)
+    p_c = dv(V.tensor_scalar(T.pc[:, :], T.pa[:, :], 48, None, A.mult))
+    m_zo = None
+    for k in range(4):
+        for bl in range(2):
+            m_zo = dv(V.tensor_scalar(T.zof[:, 16 * k + 8 * bl:16 * k + 8 * bl + 8], T.nbw[:, 8 * k:8 * k + 8],
+                                      768 * bl, None, A.add))
+            if (k, bl) == (0, 1):
+                need("V", p_c)
+                p_d = dv(V.tensor_tensor(T.pd[:, :], T.pc[:, :], T.pb[:, :], A.add))
+    need("V", p_d)
+    p_of = dv(V.tensor_copy(T.pof[:, :], T.pd[:, :]))
+    m_d0 = dv(V.memset(T.d0[:, 0:2048:4], 0.0))
+    need("V", p_of, m_inv, m_ivv)
+    m_sc = dv(V.tensor_copy(T.inv[:, 0:768].indirect(T.pof[:, 0:32]), T.ivv[:, :]))
+    need("Y", m_sc)
+    for k in range(8):
+        iv_in = done(Y.dma_start(T.invw[16 * k:16 * k + 16, :], T.inv[0:1, :]), "d_iv", 16)
+    for b in range(4):
+        m_up = dv(V.memset(T.ub[:, UW * b + 768:UW * b + UW], 0.0))
+    need("V", m_f8, m_ilp)
+    m_ilo = dv(V.tensor_scalar(T.ilo[:, :], T.ilpat[:, :], T.f8[:, :], None, A.add))
+
+    zp_free = {}
+
+    def products(half, codes, planes, st, sts, ready, who, land, wide):
+        need("P", *ready)
+        mm = []
+        for b in range(4):
+            at = 512 * (2 * b + half)
+            need("P", zp_free.get((b, half)))
+            mm.append(dp(P.matmul_mx(T.zp[:, at:at + HB], st[:, 128 * b:128 * b + 128], sts[:, 128 * b:128 * b + 128],
+                                     codes[:, HB * half:HB * half + HB], planes[:, HB * half:HB * half + HB], True, True)))
+
+        def take(b):
+            at = 512 * (2 * b + half)
+            need(who[b], mm[b])
+            out, src = land[:, wide * b + HB * half:wide * b + HB * half + HB], T.zp[:, at:at + HB]
+            m = ds(S.activation(out, src, COPY)) if who[b] == "S" else dv(V.tensor_copy(out, src))
+            zp_free[(b, half)] = m
+            return m
+        return take
+
+    zb_ok = {}
+    fa = {h: ("fa%d" % h, arrivals(r, h, cores, topo)) for h in (0, 1)}
+    take = products(ho, T.rc, T.rs, T.wq, T.ws, (w_q, fa[ho]), "SVSV", T.zb, 768)
+    for b in range(4):
+        zb_ok[(b, 0)] = take(b)
+    take = products(hr, T.rc, T.rs, T.wq, T.ws, (fa[hr], own_f), "SVVS", T.zb, 768)
+    for b in (0, 1, 2):
+        zb_ok[(b, 1)] = take(b)
+
+    def zpick(p, k):
+        return T.zb[:, 1536 * p:1536 * p + 1536].indirect(T.zof[:, 16 * k:16 * k + 16])
+
+    def seg(name, p):
+        return T[name][:, 256 * p:256 * p + 256]
+
+    z0_ok, c = {}, {}
+    for p in (0, 1):
+        if p:
+            zb_ok[(3, 1)] = take(3)
+        zready = [zb_ok[(b, i)] for b in (2 * p, 2 * p + 1) for i in (0, 1)]
+        need("S", m_zo, *zready)
+        c["z", p] = zready
+        z0_ok[p] = ds(S.activation(seg("z0", p), zpick(p, 0), COPY))
+
+    def nrec(p, k):
+        return T.d0[:, 1024 * p + 4 - k:1024 * p + 1024:4]
+
+    def vmax(p, k):
+        src, dst = (("z0", "m1"), ("m1", "m2"))[k - 1]
+        need("V", m_zo, z0_ok[p] if k == 1 else c["m1", p], *c["z", p])
+        c[dst, p] = dv(V.tensor_tensor(seg(dst, p), zpick(p, k), seg(src, p), A.max))
+
+    def vrec(p, k):
+        src = ("z0", "m1", "m2")[k - 1]
+        need("V", m_zo, m_d0, z0_ok[p] if k == 1 else c[src, p], *c["z", p])
+        c["n", p, k] = dv(V.tensor_tensor(nrec(p, k), zpick(p, k), seg(src, p), A.is_le))
+
+    def srec(p, k):
+        need("S", c["n", p, k], m_e1)
+        o = 2048 * p + 7 - 2 * k
+        c["r", p, k] = ds(S.activation(T.e0[:, o:2048 * p + 2048:8], nrec(p, k), IDENT, bias=1.0, scale=-1.0))
+
+    def scan1(p):
+        need("V", m_d0, d1_ok, m_rr, *[c["n", p, k] for k in (1, 2, 3)])
+        c["s1", p] = dv(V.tensor_tensor_scan(T.rr[:, 2048 * p:2048 * p + 2048:2], T.d0[:, 1024 * p:1024 * p + 1024],
+                                             T.d1[:, 1024 * p:1024 * p + 1024], 0.0, A.mult, A.add))
+
+    def scan2(p):
+        need("V", m_rr, m_ee, m_e1, c["s1", p], *[c["r", p, k] for k in (1, 2, 3)])
+        c["s2", p] = dv(V.tensor_tensor_scan(T.gg[:, 2048 * p:2048 * p + 2048], T.e0[:, 2048 * p:2048 * p + 2048],
+                                             T.rr[:, 2048 * p:2048 * p + 2048], 0.0, A.mult, A.add))
+
+    h_ok = {}
+
+    def place(q, b, lo, hi):
+        need(q, iv_ok[0], c["s2", b // 2])
+        out = T.h[:, 4 * lo + b:4 * hi:4]
+        src = T.gg[:, 1024 * b:1024 * b + 1024].indirect(T.ivo[:, lo // 16:hi // 16])
+        h_ok[(q, b, lo)] = ds(S.activation(out, src, COPY)) if q == "S" else dv(V.tensor_copy(out, src))
+
+    vmax(0, 1); vrec(0, 1); srec(0, 1)
+    vmax(0, 2); vrec(0, 2); srec(0, 2)
+    vrec(0, 3); srec(0, 3)
+    vmax(1, 1); scan1(0); vrec(1, 1); scan2(0)
+    need("V", iv_in)
+    iv_ok = [dv(V.tensor_copy(T.ivo[:, :], T.invw[:, :]))]
+    place("S", 0, 0, 768)
+    vmax(1, 2); srec(1, 1); vrec(1, 2); vrec(1, 3); srec(1, 2); srec(1, 3)
+    place("S", 1, 0, 768)
+    scan1(1); scan2(1)
+    for half in (ho, hr):
+        place("S", 2, HB * half, HB * half + HB)
+        place("V", 3, HB * half, HB * half + HB)
+        need("V", *h_ok.values())
+        b_q = dv(V.quantize_mx(T.bc[:, HB * half:HB * half + HB], T.bs[:, HB * half:HB * half + HB],
+                               T.h[:, 4 * HB * half:4 * HB * half + 4 * HB]))
+        need("G", b_q)
+        sends(T.bc, T.bs, T.qc, T.qs, half, "ba%d" % hr)
+    need("Y", b_q)
+    own_b = own_block(T.bc, T.bs, T.qc, T.qs, "d_ob")
+
+    need("V", m_ilo, il_in, m_ilf)
+    m_ip = dv(V.tensor_copy(T.ilp[:, :], T.ilf[:, 0:1024].indirect(T.ilo[:, 0:64])))
+    need("Y", m_ip)
+    for k in range(8):
+        ih_in = done(Y.dma_start(T.ilw[16 * k:16 * k + 16, :], T.ilp[0:1, :]), "d_ih", 16)
+    need("V", v_in)
+    v_q = dv(V.quantize_mx(T.vq[:, 0:512], T.vs[:, 0:512], T.vb[:, 0:2048]))
+    need("V", ih_in)
+    m_a = dv(V.tensor_scalar(T.ila[:, :], T.ilw[:, :], 0, 769, A.is_lt, A.mult))
+    need("V", m_a)
+    m_b = dv(V.tensor_tensor(T.ilb[:, :], T.ilw[:, :], T.ila[:, :], A.add))
+    need("V", m_b)
+    m_iq = dv(V.tensor_copy(T.ilq[:, :], T.ilb[:, :]))
+
+    ba = {h: ("ba%d" % h, arrivals(r, h, cores, topo)) for h in (0, 1)}
+    ub_ok = {}
+    take = products(ho, T.qc, T.qs, T.vq, T.vs, (v_q, ba[ho]), "SVSV", T.ub, UW)
+    for b in range(4):
+        ub_ok[(b, 0)] = take(b)
+    take = products(hr, T.qc, T.qs, T.vq, T.vs, (ba[hr], own_b), "SVSS", T.ub, UW)
+
+    def upick(b, s):
+        return T.ub[:, UW * b:UW * b + UW].indirect(T.ilq[:, 16 * s:16 * s + 16])
+
+    def blk(name, b):
+        return T[name][:, 256 * b:256 * b + 256]
+
+    acc = {}
+
+    def first(b):
+        need("S", m_iq, m_up, ub_ok[(b, 0)], ub_ok[(b, 1)])
+        acc[b] = ds(S.activation(blk("a0", b), upick(b, 0), COPY))
+
+    ub_ok[(0, 1)] = take(0); ub_ok[(1, 1)] = take(1)
+    first(0); first(1)
+    for b in (2, 3):
+        ub_ok[(b, 1)] = take(b)
+        first(b)
+    for p in (0, 1):
+        for s in (1, 2, 3):
+            for b in (2 * p, 2 * p + 1):
+                need("V", m_iq, m_up, acc[b], ub_ok[(b, 0)], ub_ok[(b, 1)])
+                acc[b] = dv(V.tensor_tensor(blk("a%d" % s, b), upick(b, s), blk("a%d" % (s - 1), b), A.add))
+        for b in (2 * p, 2 * p + 1):
+            need("V", acc[b])
+            y_ok = dv(V.tensor_tensor(T.yb[:, 128 * b:128 * b + 128], T.a3[:, 256 * b:256 * b + 128],
+                                      T.a3[:, 256 * b + 128:256 * b + 256], A.add))
+        need("Y", y_ok)
+        y_out = done(Y.dma_start(T.y[:, 256 * p:256 * p + 256], T.yb[:, 256 * p:256 * p + 256]), "d_y", 16)
+    need("Y", y_out)
+    need("G", ("ls", cnt["ls"]))

@@ -1,89 +1,74 @@
-import numpy as np
 from concourse.bass import DstId, RemoteDMATransfer
 from concourse.mybir import dt, AluOpType, ActivationFunctionType
 
-N, NT, CAP, HB = 8, 128, 96, 384
-UW = 776
+N, NT, CAP = 8, 128, 96
+ALL = N * CAP
+UW = 8 + ALL
+CW = 2 * 7 * CAP + 128
 CODES = "float8_e4m3fn_x4"
+CHUNKS = [(1,), (2, 3, 4), (5, 6, 7)]
+HELP_F = (0, 0, 192)
+HELP_B = (0, 0, 96)
+LATE = 3
 
 SCRATCH = {
     "xb": ("sbuf", [128, 528], "bfloat16"),
-    "snw": ("sbuf", [128, 48], "int32"),
-    "snof": ("sbuf", [128, 192], "uint16"),
-    "xt": ("sbuf", [128, 3072], "bfloat16"),
-    "fc": ("sbuf", [128, 768], CODES), "fs": ("sbuf", [128, 768], "uint8"),
-    "rc": ("sbuf", [128, 768], CODES), "rs": ("sbuf", [128, 768], "uint8"),
-    "wb": ("sbuf", [128, 2048], "bfloat16"),
-    "wq": ("sbuf", [128, 512], CODES), "ws": ("sbuf", [128, 512], "uint8"),
-    "vb": ("sbuf", [128, 2048], "bfloat16"),
-    "vq": ("sbuf", [128, 512], CODES), "vs": ("sbuf", [128, 512], "uint8"),
+    "snw": ("sbuf", [128, 48], "int32"), "snof": ("sbuf", [128, 192], "uint16"),
+    "xt": ("sbuf", [128, 4 * ALL], "bfloat16"),
+    "cf": ("sbuf", [128, CW], CODES), "sf": ("sbuf", [128, CW], "uint8"),
+    "cb": ("sbuf", [128, CW], CODES), "sb": ("sbuf", [128, CW], "uint8"),
+    "wb": ("sbuf", [128, 2048], "bfloat16"), "wq": ("sbuf", [128, 512], CODES), "ws": ("sbuf", [128, 512], "uint8"),
+    "vb": ("sbuf", [128, 2048], "bfloat16"), "vq": ("sbuf", [128, 512], CODES), "vs": ("sbuf", [128, 512], "uint8"),
     "zp": ("psum", [128, 4096], "float32"),
-    "zb": ("sbuf", [128, 3072], "float32"),
-    "nbd": ("dram", [16, 32], "int32"),
-    "nbw": ("sbuf", [128, 32], "int32"),
-    "zof": ("sbuf", [128, 64], "uint16"),
-    "pa": ("sbuf", [128, 32], "int32"), "pb": ("sbuf", [128, 32], "int32"),
-    "pc": ("sbuf", [128, 32], "int32"), "pd": ("sbuf", [128, 32], "int32"),
-    "pof": ("sbuf", [128, 32], "uint16"),
-    "ivv": ("sbuf", [128, 512], "int32"),
-    "inv": ("sbuf", [128, 768], "int32"),
-    "invw": ("sbuf", [128, 48], "int32"),
-    "ivo": ("sbuf", [128, 48], "uint16"),
-    "pi": ("sbuf", [128, 1], "int32"),
-    "k15": ("sbuf", [128, 1], "int32"), "k3": ("sbuf", [128, 1], "int32"), "k12": ("sbuf", [128, 1], "int32"),
-    "f8": ("sbuf", [128, 1], "float32"), "f12": ("sbuf", [128, 1], "float32"), "fgr": ("sbuf", [128, 1], "float32"),
-    "ilpat": ("sbuf", [128, 64], "int32"), "grpat": ("sbuf", [128, 32], "int32"),
-    "grb": ("sbuf", [128, 512], "bfloat16"), "gro": ("sbuf", [128, 32], "uint16"),
+    "zb": ("sbuf", [128, 4 * ALL], "float32"),
+    "nbd": ("dram", [16, 32], "int32"), "nbw": ("sbuf", [128, 32], "int32"), "zof": ("sbuf", [128, 64], "uint16"),
+    "nb8": ("sbuf", [128, 8], "int32"),
+    "pa": ("sbuf", [128, 8], "int32"), "pb": ("sbuf", [128, 8], "int32"), "pc": ("sbuf", [128, 8], "int32"),
+    "pd": ("sbuf", [128, 8], "int32"), "pof": ("sbuf", [128, 8], "uint16"),
+    "iv1": ("sbuf", [128, 128], "float32"), "iv2": ("sbuf", [128, 128], "float32"), "ivv": ("sbuf", [128, 128], "float32"),
+    "inv": ("sbuf", [128, ALL], "float32"), "invw": ("sbuf", [128, 48], "float32"), "ivo": ("sbuf", [128, 48], "uint16"),
+    "pi": ("sbuf", [128, 1], "int32"), "k15": ("sbuf", [128, 1], "int32"), "k3": ("sbuf", [128, 1], "int32"),
+    "k12": ("sbuf", [128, 1], "int32"), "f8": ("sbuf", [128, 1], "float32"), "f12": ("sbuf", [128, 1], "float32"),
+    "fgr": ("sbuf", [128, 1], "float32"),
+    "grpat": ("sbuf", [128, 32], "int32"), "gro": ("sbuf", [128, 32], "uint16"),
+    "fipat": ("sbuf", [128, 16], "int32"), "fio": ("sbuf", [128, 16], "uint16"),
+    "grb": ("sbuf", [128, 512], "bfloat16"),
     "z0": ("sbuf", [128, 512], "float32"), "m1": ("sbuf", [128, 512], "float32"), "m2": ("sbuf", [128, 512], "float32"),
-    "d0": ("sbuf", [128, 2048], "bfloat16"), "d1": ("sbuf", [128, 2048], "bfloat16"),
-    "rr": ("sbuf", [128, 4096], "bfloat16"), "e0": ("sbuf", [128, 4096], "bfloat16"),
+    "zs": ("sbuf", [128, 768], "float32"), "rs": ("sbuf", [128, 768], "float32"), "cm": ("sbuf", [128, 768], "bfloat16"),
+    "d0": ("sbuf", [128, 2048], "bfloat16"), "d1": ("sbuf", [128, 1024], "bfloat16"),
+    "ca": ("sbuf", [128, 1024], "bfloat16"), "cs8": ("sbuf", [128, 1024], "bfloat16"),
     "gg": ("sbuf", [128, 4096], "bfloat16"),
-    "h": ("sbuf", [128, 3072], "bfloat16"),
-    "bc": ("sbuf", [128, 768], CODES), "bs": ("sbuf", [128, 768], "uint8"),
-    "qc": ("sbuf", [128, 768], CODES), "qs": ("sbuf", [128, 768], "uint8"),
+    "h": ("sbuf", [128, 4 * ALL], "bfloat16"),
     "ub": ("sbuf", [128, 4 * UW], "float32"),
-    "ilf": ("sbuf", [128, 1024], "int32"), "ilo": ("sbuf", [128, 64], "uint16"),
-    "ilp": ("sbuf", [128, 1024], "int32"), "ilw": ("sbuf", [128, 64], "int32"),
-    "ila": ("sbuf", [128, 64], "int32"), "ilb": ("sbuf", [128, 64], "int32"),
-    "ilq": ("sbuf", [128, 64], "uint16"),
-    "a0": ("sbuf", [128, 1024], "float32"), "a1": ("sbuf", [128, 1024], "float32"),
-    "a2": ("sbuf", [128, 1024], "float32"), "a3": ("sbuf", [128, 1024], "float32"),
-    "yb": ("sbuf", [128, 512], "float32"),
+    "ild": ("dram", [16, 128], "int32"), "ilw": ("sbuf", [128, 128], "int32"), "ilq": ("sbuf", [128, 128], "uint16"),
+    "acc": ("sbuf", [128, 4096], "float32"), "sum": ("sbuf", [128, 4096], "float32"),
+    "fin": ("sbuf", [128, 512], "float32"), "yb": ("sbuf", [128, 512], "float32"),
 }
-SEMAPHORES = ["cv", "cs", "ct", "cp", "d_x", "d_sn", "d_w", "d_v", "d_gr", "d_nd", "d_nb", "d_il", "d_iv", "d_ih",
-              "d_of", "d_ob", "d_y", "fa0", "fa1", "ba0", "ba1", "ls"]
+SEMAPHORES = ["cv", "cs", "ct", "cp", "d_x", "d_sn", "d_w", "d_v", "d_gr", "d_nd", "d_nb", "d_n8", "d_id", "d_il",
+              "d_add", "d_ad2", "d_iv", "d_y", "f0", "f1", "b0", "b1", "ls"]
 
 
-def half_sends(s, half, cores, topo):
-    ds = [d for d in range(4 * half, 4 * half + 4) if d != s]
-    if len(ds) == 4:
-        cut_c = cut_p = [(0, 2), (2, 4), (4, 6), (6, 8)]
-    else:
-        cut_c, cut_p = [(0, 4), (4, 6), (6, 8)], [(0, 2), (2, 4), (4, 8)]
-    out = []
-    for d, (a, b), (u, v) in zip(ds, cut_c, cut_p):
-        e = topo.engines(cores[s], cores[d])
-        out.append((d, e[a:b], e[u:v]))
-    return out
+def way(ph, s, j):
+    if ph == "f":
+        return (s - j) % N, CAP * (7 - j), 7 * CAP + 128 + CAP * (j - 1)
+    return (s + j) % N, 7 * CAP + 128 + CAP * (j - 1), CAP * (7 - j)
 
 
-def arrivals(r, half, cores, topo):
-    n = 0
-    for s in range(4 * half, 4 * half + 4):
-        if s != r:
-            for d, ec, ep in half_sends(s, r // 4, cores, topo):
-                if d == r:
-                    n += len(ec) + len(ep)
-    return n
+def shares(n, flip):
+    s = {1: [8], 2: [4, 4], 3: [4, 2, 2], 4: [2, 2, 2, 2]}[n]
+    return s[::-1] if flip else s
+
+
+def group_of(j):
+    return 1 if j > 7 - LATE else 0
 
 
 def rank_program(g, core, T, topo):
     r = T.rank_of(core)
     if r is None:
         return
-    A, COPY, IDENT = AluOpType, ActivationFunctionType.Copy, ActivationFunctionType.Identity
     cores = list(T.cores)
-    hr, ho = r // 4, 1 - r // 4
+    A, COPY = AluOpType, ActivationFunctionType.Copy
     V, S, P, Y = g.vector, g.scalar, g.tensor, g.sync
     qn = {"V": V, "S": S, "P": P, "Y": Y, "G": g}
     cnt, seen = {}, {}
@@ -96,8 +81,7 @@ def rank_program(g, core, T, topo):
     def need(q, *marks):
         best = {}
         for m in marks:
-            if m is not None:
-                best[m[0]] = max(best.get(m[0], 0), m[1])
+            best[m[0]] = max(best.get(m[0], 0), m[1])
         for sem, val in best.items():
             if seen.get((q, sem), 0) < val:
                 qn[q].wait_ge(T.sem[sem], val)
@@ -105,270 +89,313 @@ def rank_program(g, core, T, topo):
 
     def dv(ins): return done(ins, "cv")
     def ds(ins): return done(ins, "cs")
-    def dp(ins): return done(ins, "ct")
     def dg(ins): return done(ins, "cp")
 
+    def move(q, out, src, *marks):
+        need(q, *marks)
+        return ds(S.activation(out, src, COPY)) if q == "S" else dv(V.tensor_copy(out, src))
+
+    def runs(first, n):
+        first %= N
+        k = min(n, N - first)
+        return [(0, first, k)] + ([(k, 0, n - k)] if k < n else [])
+
+    def iota(out, pattern, base=0, step=0):
+        return dg(g.iota(out, pattern, base, step, allow_small_or_imprecise_dtypes=True))
+
     x_in = done(S.dma_start(T.xb[:, 16:528], T.x[:, :]), "d_x", 16)
-    for k in range(5):
-        done(Y.dma_start(T.snw[16 * k:16 * k + 16, :], T.sn[:, :]), "d_sn", 16)
-    for k in range(5, 8):
-        sn_in = done(S.dma_start(T.snw[16 * k:16 * k + 16, :], T.sn[:, :]), "d_sn", 16)
+    for k in range(8):
+        sn_in = done((Y if k < 5 else S).dma_start(T.snw[16 * k:16 * k + 16, :], T.sn[:, :]), "d_sn", 16)
     for k in range(4):
         nd_in = done(Y.dma_start(T.nbd[:, 8 * k:8 * k + 8], T.nb[k:16:4, :]), "d_nd", 16)
+    for k in range(2):
+        n8_in = done(S.dma_start(T.nb8[64 * k:64 * k + 64, :], T.nb[:, :]), "d_n8", 16)
     w_in = done(Y.dma_start(T.wb[:, :], T.w[:, :]), "d_w", 16)
     gr_in = done(S.dma_start(T.grb[:, :], T.gr[:, :]), "d_gr", 16)
     need("Y", nd_in)
     for k in range(8):
         nb_in = done(Y.dma_start(T.nbw[16 * k:16 * k + 16, :], T.nbd[:, :]), "d_nb", 16)
-    v_in = done(Y.dma_start(T.vb[:, :], T.w2[:, :]), "d_v", 16)
 
     m_pi = dg(g.iota(T.pi[:, :], [[0, 1]], 0, 1))
-    m_grp = dg(g.iota(T.grpat[:, :], [[1, 4], [16, 8]], 0, 0))
-    m_ivv = dg(g.iota(T.ivv[:, :], [[-2, 4], [8, 128]], 7, 0))
-    m_ilp = dg(g.iota(T.ilpat[:, :], [[1, 8], [512, 2], [128, 4]], 0, 0))
+    m_grp = dg(g.iota(T.grpat[:, :], [[2, 2], [16, 8], [1, 2]], 0, 0))
+    iota(T.iv1[:, :], [[128, 8], [-2, 2], [0, 8]], 3, 1)
+    m_iv = iota(T.iv2[:, :], [[0, 16], [1024, 2], [4, 4]])
 
     m_pad = dv(V.memset(T.xb[:, 0:16], 0.0))
-    need("V", m_pi)
-    k15 = dv(V.tensor_scalar(T.k15[:, :], T.pi[:, :], 15, None, A.bitwise_and))
-    k3 = dv(V.tensor_scalar(T.k3[:, :], T.pi[:, :], 3, None, A.bitwise_and))
-    k12 = dv(V.tensor_scalar(T.k12[:, :], T.pi[:, :], 12, None, A.bitwise_and))
-    m_ilf = dv(V.memset(T.ilf[:, :], 0))
-    m_inv = dv(V.memset(T.inv[:, :], 0))
-    need("V", k12)
-    m_f8 = dv(V.tensor_scalar(T.f8[:, :], T.k15[:, :], 8, None, A.mult))
-    m_f12 = dv(V.tensor_copy(T.f12[:, :], T.k12[:, :]))
-    need("Y", m_ilf)
-    il_in = done(Y.dma_start(T.ilf[0:1, :], T.il[:, :]), "d_il", 16)
+    m_inv = dv(V.memset(T.inv[:, :], 0.0))
+    m_d1 = dv(V.memset(T.d1[:, :], 0.0))
+
+    arrived = {}
+
+    def send(ph, codes, planes, i):
+        for buf in (codes, planes):
+            tr, k = [], 0
+            for j, n in zip(CHUNKS[i], shares(len(CHUNKS[i]), (buf is planes) != (i % 2 == 0))):
+                d, a, b = way(ph, r, j)
+                rid, pid, _ = topo.addr(cores[d])
+                x, y = buf[:, a:a + CAP], buf[:, b:b + CAP]
+                if buf is codes:
+                    x, y = x.bitcast(dt.uint8), y.bitcast(dt.uint8)
+                sem = ph + str(group_of(j))
+                tr.append(RemoteDMATransfer(dst_ids=[DstId(rid=rid, pnc=pid)],
+                                            dma_engine_mask=sum(1 << e for e in topo.engines(core, cores[d])[k:k + n]),
+                                            remote_sem=T.sem[sem], srcs=[x], dsts=[y]))
+                k += n
+                arrived[sem] = (sem, arrived.get(sem, (sem, 0))[1] + n)
+            g.remote_dma_fused(tr, local_sem=T.sem["ls"])
+            cnt["ls"] = cnt.get("ls", 0) + k
 
     need("V", sn_in)
-    snof = []
-    for t in range(4):
-        snof.append(dv(V.tensor_scalar(T.snof[:, 48 * t:48 * t + 48], T.snw[:, :], 4, 16 + t, A.mult, A.add)))
+    snof = [dv(V.tensor_scalar(T.snof[:, 48 * t:48 * t + 48], T.snw[:, :], 4, 16 + t, A.mult, A.add)) for t in range(4)]
+    turn = CAP * (N - 1 - r)
 
-    def sends(codes, planes, lc, lp, half, sem):
-        for own, land, w in ((codes, lc, 0), (planes, lp, 1)):
-            tr = []
-            for d, ec, ep in half_sends(r, half, cores, topo):
-                rid, pid, _ = topo.addr(cores[d])
-                mask = sum(1 << e for e in (ep if w else ec))
-                src, dst = own[:, CAP * d:CAP * d + CAP], land[:, CAP * r:CAP * r + CAP]
-                if not w:
-                    src, dst = src.bitcast(dt.uint8), dst.bitcast(dt.uint8)
-                tr.append(RemoteDMATransfer(dst_ids=[DstId(rid=rid, pnc=pid)], dma_engine_mask=mask,
-                                            remote_sem=T.sem[sem], srcs=[src], dsts=[dst]))
-                cnt["ls"] = cnt.get("ls", 0) + len(ep if w else ec)
-            g.remote_dma_fused(tr, local_sem=T.sem["ls"])
-
-    def own_block(codes, planes, lc, lp, sem):
-        a, b = CAP * r, CAP * r + CAP
-        done(Y.dma_start(lc[:, a:b].bitcast(dt.uint8), codes[:, a:b].bitcast(dt.uint8)), sem, 16)
-        return done(Y.dma_start(lp[:, a:b], planes[:, a:b]), sem, 16)
-
-    for half in (ho, hr):
-        win = T.xb[:, 0:528]
+    def pick_x(who, lo, hi):
         marks = []
-        for q, t in (("S", 0), ("V", 2), ("S", 1), ("V", 3)):
-            need(q, x_in, m_pad, snof[t])
-            out = T.xt[:, 4 * HB * half + t:4 * HB * (half + 1):4]
-            src = win.indirect(T.snof[:, 48 * t + 24 * half:48 * t + 24 * half + 24])
-            marks.append(ds(S.activation(out, src, COPY)) if q == "S" else dv(V.tensor_copy(out, src)))
+        for t in sorted(range(4), key=lambda t: (who[:t].count(who[t]), t)):
+            for a, b in ((lo, min(hi, turn)), (max(lo, turn), hi)):
+                if a < b and who[t] != ".":
+                    e = 48 * t + (a + CAP * (r + 1)) % ALL // 16
+                    marks.append(move(who[t], T.xt[:, 4 * a + t:4 * b:4],
+                                      T.xb[:, 0:528].indirect(T.snof[:, e:e + (b - a) // 16]), x_in, m_pad, snof[t]))
+        return marks
+
+    def quantise(codes, planes, at, tile, lo, hi, marks):
         need("V", *marks)
-        f_q = dv(V.quantize_mx(T.fc[:, HB * half:HB * half + HB], T.fs[:, HB * half:HB * half + HB],
-                               T.xt[:, 4 * HB * half:4 * HB * half + 4 * HB]))
-        need("G", f_q)
-        sends(T.fc, T.fs, T.rc, T.rs, half, "fa%d" % hr)
-    need("Y", f_q)
-    own_f = own_block(T.fc, T.fs, T.rc, T.rs, "d_of")
+        return dv(V.quantize_mx(codes[:, at:at + hi - lo], planes[:, at:at + hi - lo], tile[:, 4 * lo:4 * hi]))
 
-    m_rr = dg(g.iota(T.rr[:, 1:4096:2], [[0, 2048]], 0, 0, allow_small_or_imprecise_dtypes=True))
-    m_ee = dg(g.iota(T.e0[:, 0:4096:2], [[0, 2048]], 0, 0, allow_small_or_imprecise_dtypes=True))
-    m_e1 = dg(g.iota(T.e0[:, 7:4096:8], [[0, 512]], 1, 0, allow_small_or_imprecise_dtypes=True))
+    spare = max(0, 128 - CAP * len(CHUNKS[0]))
+    below, above = (spare, 0) if turn == 7 * CAP else (0, spare)
+    f_q = []
+    for i, steps in enumerate(CHUNKS):
+        lo, hi = CAP * (7 - steps[-1]), CAP * (8 - steps[0])
+        if i == 0:
+            lo, hi = lo - below, hi + above
+        top = hi - (below if i == 1 else 0)
+        if HELP_F[i]:
+            marks = pick_x("SS.V", lo, top) + pick_x("..V.", lo, top - HELP_F[i]) + pick_x("..S.", top - HELP_F[i], top)
+        else:
+            marks = pick_x("SSVV", lo, top)
+        f_q = [quantise(T.cf, T.sf, lo, T.xt, lo, hi, marks + (f_q if below else []))]
+        need("G", *f_q)
+        send("f", T.cf, T.sf, i)
+    own = pick_x("SSSS", 7 * CAP + above, ALL)
 
-    m_d1 = dv(V.memset(T.d1[:, :], 0.0))
-    need("V", m_f12, k3)
-    m_fgr = dv(V.tensor_scalar(T.fgr[:, :], T.k3[:, :], 128, T.f12[:, :], A.mult, A.add))
     need("V", w_in)
     w_q = dv(V.quantize_mx(T.wq[:, 0:512], T.ws[:, 0:512], T.wb[:, 0:2048]))
-    need("V", m_fgr, m_grp)
-    m_gro = dv(V.tensor_scalar(T.gro[:, :], T.grpat[:, :], T.fgr[:, :], None, A.add))
-    need("S", m_d1, m_gro, gr_in)
-    d1_ok = ds(S.activation(T.d1[:, 0:2048:4], T.grb[:, 0:512].indirect(T.gro[:, 0:32]), COPY))
-
-    need("V", nb_in)
-    p_a = dv(V.tensor_scalar(T.pa[:, :], T.nbw[:, :], 15, None, A.bitwise_and))
-    p_b = dv(V.tensor_scalar(T.pb[:, :], T.nbw[:, :], 4, None, A.arith_shift_right))
+    own_f = quantise(T.cf, T.sf, 7 * CAP, T.xt, ALL - 128, ALL, own + f_q)
+    need("V", n8_in, m_pi)
+    p_a = dv(V.tensor_scalar(T.pa[:, :], T.nb8[:, :], 15, None, A.bitwise_and))
+    p_b = dv(V.tensor_scalar(T.pb[:, :], T.nb8[:, :], 4, None, A.arith_shift_right))
+    k12 = dv(V.tensor_scalar(T.k12[:, :], T.pi[:, :], 12, None, A.bitwise_and))
     need("V", p_a)
     p_c = dv(V.tensor_scalar(T.pc[:, :], T.pa[:, :], 48, None, A.mult))
-    m_zo = None
-    for k in range(4):
-        for bl in range(2):
-            m_zo = dv(V.tensor_scalar(T.zof[:, 16 * k + 8 * bl:16 * k + 8 * bl + 8], T.nbw[:, 8 * k:8 * k + 8],
-                                      768 * bl, None, A.add))
-            if (k, bl) == (0, 1):
-                need("V", p_c)
-                p_d = dv(V.tensor_tensor(T.pd[:, :], T.pc[:, :], T.pb[:, :], A.add))
+    need("V", m_iv)
+    m_ivv = dv(V.tensor_tensor(T.ivv[:, :], T.iv1[:, :], T.iv2[:, :], A.add))
+    need("V", p_c, p_b)
+    p_d = dv(V.tensor_tensor(T.pd[:, :], T.pc[:, :], T.pb[:, :], A.add))
+    need("V", nb_in)
+    for bl in range(2):
+        m_zo = dv(V.tensor_scalar(T.zof[:, bl:64:2], T.nbw[:, :], ALL * bl, None, A.add))
     need("V", p_d)
     p_of = dv(V.tensor_copy(T.pof[:, :], T.pd[:, :]))
-    m_d0 = dv(V.memset(T.d0[:, 0:2048:4], 0.0))
+    k3 = dv(V.tensor_scalar(T.k3[:, :], T.pi[:, :], 3, None, A.bitwise_and))
+    need("V", k12)
+    m_f12 = dv(V.tensor_copy(T.f12[:, :], T.k12[:, :]))
     need("V", p_of, m_inv, m_ivv)
-    m_sc = dv(V.tensor_copy(T.inv[:, 0:768].indirect(T.pof[:, 0:32]), T.ivv[:, :]))
-    need("Y", m_sc)
+    m_sc = dv(V.tensor_copy(T.inv[:, 0:ALL].indirect(T.pof[:, 0:8]), T.ivv[:, :]))
+    need("V", m_f12, k3)
+    m_fgr = dv(V.tensor_scalar(T.fgr[:, :], T.k3[:, :], 128, T.f12[:, :], A.mult, A.add))
+    m_cm = [dv(V.memset(T.cm[:, k:768:3], 0.0 if k else -1e29)) for k in range(3)]
+    need("V", m_fgr, m_grp)
+    m_gro = dv(V.tensor_scalar(T.gro[:, :], T.grpat[:, :], T.fgr[:, :], None, A.add))
+
+    def lay_gr(p, *marks):
+        return move("S", T.d1[:, 0:1024:4], T.grb[:, 0:512].indirect(T.gro[:, 16 * p:16 * p + 16]), m_gro, gr_in, *marks)
+
+    need("G", m_sc)
+    done(g.dma_start(T.inv[0:1, :], T.inv[32:33, :], accum_op=A.add), "d_add", 16)
+    add = done(g.dma_start(T.inv[16:17, :], T.inv[48:49, :], accum_op=A.add), "d_add", 16)
+    m_d0 = iota(T.d0[:, 0:2048:4], [[0, 512]])
+    need("G", add)
+    added = done(g.dma_start(T.inv[0:1, :], T.inv[16:17, :], accum_op=A.add), "d_ad2", 16)
+    m_ca = iota(T.ca[:, :], [[0, 512], [-1, 2]])
+    for b in range(4):
+        m_up = iota(T.ub[:, UW * b:UW * b + 8], [[0, 8]])
+    m_fip = dg(g.iota(T.fipat[:, :], [[4, 2], [1, 4], [128, 2]], 0, 0))
+    m_c1 = iota(T.cs8[:, :], [[0, 1024]], 1)
+    need("G", m_c1)
+    m_cs = iota(T.cs8[:, 0:1024:8], [[0, 128]])
+
+    need("Y", arrived["f1"])
+    v_in = done(Y.dma_start(T.vb[:, :], T.w2[:, :]), "d_v", 16)
+    for s in range(4):
+        done(Y.dma_start(T.ild[:, 16 * s:16 * s + 16], T.il[s:16:4, :]), "d_id", 16)
+    id_in = done(Y.dma_start(T.ild[:, 64:128], T.il[:, :]), "d_id", 16)
+    need("Y", added)
     for k in range(8):
         iv_in = done(Y.dma_start(T.invw[16 * k:16 * k + 16, :], T.inv[0:1, :]), "d_iv", 16)
-    for b in range(4):
-        m_up = dv(V.memset(T.ub[:, UW * b + 768:UW * b + UW], 0.0))
-    need("V", m_f8, m_ilp)
-    m_ilo = dv(V.tensor_scalar(T.ilo[:, :], T.ilpat[:, :], T.f8[:, :], None, A.add))
+    need("Y", id_in)
+    for k in range(8):
+        il_in = done(Y.dma_start(T.ilw[16 * k:16 * k + 16, :], T.ild[:, :]), "d_il", 16)
 
     zp_free = {}
 
-    def products(half, codes, planes, st, sts, ready, who, land, wide):
+    def products(grp, codes, planes, lo, first, n, st, sts, ready, land, wide, pad):
         need("P", *ready)
         mm = []
         for b in range(4):
-            at = 512 * (2 * b + half)
-            need("P", zp_free.get((b, half)))
-            mm.append(dp(P.matmul_mx(T.zp[:, at:at + HB], st[:, 128 * b:128 * b + 128], sts[:, 128 * b:128 * b + 128],
-                                     codes[:, HB * half:HB * half + HB], planes[:, HB * half:HB * half + HB], True, True)))
+            at = 512 * (2 * b + grp)
+            need("P", *zp_free.get((b, grp), []))
+            mm.append(done(P.matmul_mx(T.zp[:, at:at + CAP * n], st[:, 128 * b:128 * b + 128], sts[:, 128 * b:128 * b + 128],
+                                       codes[:, lo:lo + CAP * n], planes[:, lo:lo + CAP * n], True, True), "ct"))
 
-        def take(b):
-            at = 512 * (2 * b + half)
-            need(who[b], mm[b])
-            out, src = land[:, wide * b + HB * half:wide * b + HB * half + HB], T.zp[:, at:at + HB]
-            m = ds(S.activation(out, src, COPY)) if who[b] == "S" else dv(V.tensor_copy(out, src))
-            zp_free[(b, half)] = m
-            return m
+        def take(q, b):
+            at, to = 512 * (2 * b + grp), wide * b + pad
+            zp_free[(b, grp)] = [move(q, land[:, to + CAP * d:to + CAP * (d + k)], T.zp[:, at + CAP * o:at + CAP * (o + k)],
+                                      mm[b]) for o, d, k in runs(first, n)]
+            return zp_free[(b, grp)]
         return take
 
-    zb_ok = {}
-    fa = {h: ("fa%d" % h, arrivals(r, h, cores, topo)) for h in (0, 1)}
-    take = products(ho, T.rc, T.rs, T.wq, T.ws, (w_q, fa[ho]), "SVSV", T.zb, 768)
-    for b in range(4):
-        zb_ok[(b, 0)] = take(b)
-    take = products(hr, T.rc, T.rs, T.wq, T.ws, (fa[hr], own_f), "SVVS", T.zb, 768)
-    for b in (0, 1, 2):
-        zb_ok[(b, 1)] = take(b)
+    zb_ok = {b: [] for b in range(4)}
+    take = products(0, T.cf, T.sf, 7 * CAP + 32, r, N - LATE, T.wq, T.ws, (w_q, own_f, arrived["f0"]), T.zb, ALL, 0)
+    for q, b in zip("SSVS", range(4)):
+        zb_ok[b] += take(q, b)
+    take = products(1, T.cf, T.sf, CW - CAP * LATE, r - LATE, LATE, T.wq, T.ws, (arrived["f1"],), T.zb, ALL, 0)
+    zb_ok[0] += take("S", 0)
+    zb_ok[1] += take("V", 1)
 
-    def zpick(p, k):
-        return T.zb[:, 1536 * p:1536 * p + 1536].indirect(T.zof[:, 16 * k:16 * k + 16])
+    def zpick(p, k, lo=0, hi=16):
+        return T.zb[:, 2 * ALL * p:2 * ALL * (p + 1)].indirect(T.zof[:, 16 * k + lo:16 * k + hi])
 
     def seg(name, p):
         return T[name][:, 256 * p:256 * p + 256]
 
-    z0_ok, c = {}, {}
-    for p in (0, 1):
-        if p:
-            zb_ok[(3, 1)] = take(3)
-        zready = [zb_ok[(b, i)] for b in (2 * p, 2 * p + 1) for i in (0, 1)]
-        need("S", m_zo, *zready)
-        c["z", p] = zready
-        z0_ok[p] = ds(S.activation(seg("z0", p), zpick(p, 0), COPY))
+    c = {}
+    c["z0", 0] = [move("S", T.z0[:, 0:128], zpick(0, 0, 0, 8), m_zo, *zb_ok[0], *zb_ok[1]),
+                  move("V", T.z0[:, 128:256], zpick(0, 0, 8, 16), m_zo, *zb_ok[0], *zb_ok[1])]
+    zb_ok[2] += take("S", 2)
+    zb_ok[3] += take("S", 3)
+    d1_ok = {0: lay_gr(0, m_d1)}
+    c["zs"] = [move("S", T.zs[:, k:768:3], zpick(1, k), *zb_ok[2], *zb_ok[3]) for k in range(3)]
 
-    def nrec(p, k):
-        return T.d0[:, 1024 * p + 4 - k:1024 * p + 1024:4]
+    def running():
+        need("V", *c["zs"], *m_cm)
+        c["rs"] = dv(V.tensor_tensor_scan(T.rs[:, :], T.cm[:, :], T.zs[:, :], 0.0, A.add, A.max))
 
     def vmax(p, k):
         src, dst = (("z0", "m1"), ("m1", "m2"))[k - 1]
-        need("V", m_zo, z0_ok[p] if k == 1 else c["m1", p], *c["z", p])
-        c[dst, p] = dv(V.tensor_tensor(seg(dst, p), zpick(p, k), seg(src, p), A.max))
+        need("V", *c[src, p])
+        c[dst, p] = [dv(V.tensor_tensor(seg(dst, p), zpick(p, k), seg(src, p), A.max))]
 
     def vrec(p, k):
         src = ("z0", "m1", "m2")[k - 1]
-        need("V", m_zo, m_d0, z0_ok[p] if k == 1 else c[src, p], *c["z", p])
-        c["n", p, k] = dv(V.tensor_tensor(nrec(p, k), zpick(p, k), seg(src, p), A.is_le))
+        need("V", *(c[src, p] if p == 0 else [c["rs"]]))
+        c["n", p, k] = dv(V.tensor_tensor(T.d0[:, 1024 * p + 4 - k:1024 * p + 1024:4], zpick(p, k),
+                                          seg(src, p) if p == 0 else T.rs[:, k - 1:768:3], A.is_le))
 
-    def srec(p, k):
-        need("S", c["n", p, k], m_e1)
-        o = 2048 * p + 7 - 2 * k
-        c["r", p, k] = ds(S.activation(T.e0[:, o:2048 * p + 2048:8], nrec(p, k), IDENT, bias=1.0, scale=-1.0))
+    def keep(p):
+        need("V", m_d0, d1_ok[p], *[c["n", p, k] for k in (1, 2, 3)])
+        c["k", p] = dv(V.tensor_tensor_scan(T.gg[:, 2048 * p:2048 * p + 1024], T.d0[:, 1024 * p:1024 * p + 1024],
+                                            T.d1[:, :], 0.0, A.mult, A.add))
 
-    def scan1(p):
-        need("V", m_d0, d1_ok, m_rr, *[c["n", p, k] for k in (1, 2, 3)])
-        c["s1", p] = dv(V.tensor_tensor_scan(T.rr[:, 2048 * p:2048 * p + 2048:2], T.d0[:, 1024 * p:1024 * p + 1024],
-                                             T.d1[:, 1024 * p:1024 * p + 1024], 0.0, A.mult, A.add))
+    def odd(p):
+        need("V", m_ca, c["k", p])
+        c["a", p] = dv(V.tensor_tensor_scan(T.gg[:, 2048 * p + 1024:2048 * p + 2048], T.ca[:, :],
+                                            T.gg[:, 2048 * p:2048 * p + 1024], 0.0, A.mult, A.subtract))
 
-    def scan2(p):
-        need("V", m_rr, m_ee, m_e1, c["s1", p], *[c["r", p, k] for k in (1, 2, 3)])
-        c["s2", p] = dv(V.tensor_tensor_scan(T.gg[:, 2048 * p:2048 * p + 2048], T.e0[:, 2048 * p:2048 * p + 2048],
-                                             T.rr[:, 2048 * p:2048 * p + 2048], 0.0, A.mult, A.add))
-
-    h_ok = {}
+    def second(p):
+        need("V", c["a", p])
+        k2 = T.gg[:, 2048 * p + 1:2048 * p + 1024:4]
+        c["g", p] = dv(V.tensor_tensor(k2, k2, T.gg[:, 2048 * p + 2:2048 * p + 1024:4], A.subtract))
 
     def place(q, b, lo, hi):
-        need(q, iv_ok[0], c["s2", b // 2])
-        out = T.h[:, 4 * lo + b:4 * hi:4]
-        src = T.gg[:, 1024 * b:1024 * b + 1024].indirect(T.ivo[:, lo // 16:hi // 16])
-        h_ok[(q, b, lo)] = ds(S.activation(out, src, COPY)) if q == "S" else dv(V.tensor_copy(out, src))
+        p, bl = divmod(b, 2)
+        return move(q, T.h[:, 4 * lo + b:4 * hi:4],
+                    T.gg[:, 2048 * p + 64 * bl:2048 * p + 2048].indirect(T.ivo[:, lo // 16:hi // 16]), c["g", p], *iv_ok)
 
-    vmax(0, 1); vrec(0, 1); srec(0, 1)
-    vmax(0, 2); vrec(0, 2); srec(0, 2)
-    vrec(0, 3); srec(0, 3)
-    vmax(1, 1); scan1(0); vrec(1, 1); scan2(0)
+    vmax(0, 1); vrec(0, 1); vmax(0, 2); vrec(0, 2); vrec(0, 3)
+    keep(0); running(); odd(0)
+    d1_ok[1] = lay_gr(1, c["k", 0])
     need("V", iv_in)
-    iv_ok = [dv(V.tensor_copy(T.ivo[:, :], T.invw[:, :]))]
-    place("S", 0, 0, 768)
-    vmax(1, 2); srec(1, 1); vrec(1, 2); vrec(1, 3); srec(1, 2); srec(1, 3)
-    place("S", 1, 0, 768)
-    scan1(1); scan2(1)
-    for half in (ho, hr):
-        place("S", 2, HB * half, HB * half + HB)
-        place("V", 3, HB * half, HB * half + HB)
-        need("V", *h_ok.values())
-        b_q = dv(V.quantize_mx(T.bc[:, HB * half:HB * half + HB], T.bs[:, HB * half:HB * half + HB],
-                               T.h[:, 4 * HB * half:4 * HB * half + 4 * HB]))
+    iv_ok = [dv(V.tensor_copy(T.ivo[:, 6 * o:6 * (o + k)], T.invw[:, 6 * d:6 * (d + k)])) for o, d, k in runs(r, N)]
+    second(0)
+    h_ok = [place("S", 0, 0, ALL), place("S", 1, 0, ALL)]
+    vrec(1, 1); vrec(1, 2); vrec(1, 3); keep(1); odd(1); second(1)
+    for i, steps in enumerate(CHUNKS):
+        lo, hi = CAP * steps[0] - (spare if i == 0 else 0), CAP * (steps[-1] + 1)
+        cut = hi - HELP_B[i]
+        marks = [place("S", 2, lo, hi), place("V", 3, lo, cut)] + ([place("S", 3, cut, hi)] if cut < hi else [])
+        b_q = quantise(T.cb, T.sb, 7 * CAP + 32 + lo, T.h, lo, hi, marks + h_ok)
         need("G", b_q)
-        sends(T.bc, T.bs, T.qc, T.qs, half, "ba%d" % hr)
-    need("Y", b_q)
-    own_b = own_block(T.bc, T.bs, T.qc, T.qs, "d_ob")
+        send("b", T.cb, T.sb, i)
+    own = [place("S", 2, 0, CAP - spare), place("S", 3, 0, CAP - spare)]
 
-    need("V", m_ilo, il_in, m_ilf)
-    m_ip = dv(V.tensor_copy(T.ilp[:, :], T.ilf[:, 0:1024].indirect(T.ilo[:, 0:64])))
-    need("Y", m_ip)
-    for k in range(8):
-        ih_in = done(Y.dma_start(T.ilw[16 * k:16 * k + 16, :], T.ilp[0:1, :]), "d_ih", 16)
     need("V", v_in)
     v_q = dv(V.quantize_mx(T.vq[:, 0:512], T.vs[:, 0:512], T.vb[:, 0:2048]))
-    need("V", ih_in)
-    m_a = dv(V.tensor_scalar(T.ila[:, :], T.ilw[:, :], 0, 769, A.is_lt, A.mult))
-    need("V", m_a)
-    m_b = dv(V.tensor_tensor(T.ilb[:, :], T.ilw[:, :], T.ila[:, :], A.add))
-    need("V", m_b)
-    m_iq = dv(V.tensor_copy(T.ilq[:, :], T.ilb[:, :]))
+    own_b = quantise(T.cb, T.sb, 7 * CAP, T.h, 0, 128, own + [b_q])
+    k15 = dv(V.tensor_scalar(T.k15[:, :], T.pi[:, :], 15, None, A.bitwise_and))
+    need("V", il_in)
+    m_iq = dv(V.tensor_scalar(T.ilq[:, :], T.ilw[:, :], 8, None, A.add))
+    need("V", k15)
+    m_f8 = dv(V.tensor_scalar(T.f8[:, :], T.k15[:, :], 8, None, A.mult))
+    need("V", m_f8, m_fip)
+    m_fio = dv(V.tensor_scalar(T.fio[:, :], T.fipat[:, :], T.f8[:, :], None, A.add))
 
-    ba = {h: ("ba%d" % h, arrivals(r, h, cores, topo)) for h in (0, 1)}
-    ub_ok = {}
-    take = products(ho, T.qc, T.qs, T.vq, T.vs, (v_q, ba[ho]), "SVSV", T.ub, UW)
-    for b in range(4):
-        ub_ok[(b, 0)] = take(b)
-    take = products(hr, T.qc, T.qs, T.vq, T.vs, (ba[hr], own_b), "SVSS", T.ub, UW)
+    ub_ok = {b: [m_iq, m_up] for b in range(4)}
+    take = products(0, T.cb, T.sb, CAP * LATE, r + 1 + LATE, N - LATE, T.vq, T.vs, (v_q, own_b, arrived["b0"]), T.ub, UW, 8)
+    for q, b in zip("SVSV", range(4)):
+        ub_ok[b] += take(q, b)
+    take = products(1, T.cb, T.sb, 0, r + 1, LATE, T.vq, T.vs, (arrived["b1"],), T.ub, UW, 8)
 
-    def upick(b, s):
-        return T.ub[:, UW * b:UW * b + UW].indirect(T.ilq[:, 16 * s:16 * s + 16])
+    def upick(b, lo, hi):
+        return T.ub[:, UW * b:UW * b + UW].indirect(T.ilq[:, lo:hi])
 
-    def blk(name, b):
-        return T[name][:, 256 * b:256 * b + 256]
+    def part(name, b, s, n=256):
+        return T[name][:, 1024 * b + n * s:1024 * b + n * (s + 1)]
 
-    acc = {}
+    a = {}
 
-    def first(b):
-        need("S", m_iq, m_up, ub_ok[(b, 0)], ub_ok[(b, 1)])
-        acc[b] = ds(S.activation(blk("a0", b), upick(b, 0), COPY))
+    def copy(q, b):
+        ub_ok[b] += take(q, b)
 
-    ub_ok[(0, 1)] = take(0); ub_ok[(1, 1)] = take(1)
-    first(0); first(1)
-    for b in (2, 3):
-        ub_ok[(b, 1)] = take(b)
-        first(b)
-    for p in (0, 1):
-        for s in (1, 2, 3):
-            for b in (2 * p, 2 * p + 1):
-                need("V", m_iq, m_up, acc[b], ub_ok[(b, 0)], ub_ok[(b, 1)])
-                acc[b] = dv(V.tensor_tensor(blk("a%d" % s, b), upick(b, s), blk("a%d" % (s - 1), b), A.add))
-        for b in (2 * p, 2 * p + 1):
-            need("V", acc[b])
-            y_ok = dv(V.tensor_tensor(T.yb[:, 128 * b:128 * b + 128], T.a3[:, 256 * b:256 * b + 128],
-                                      T.a3[:, 256 * b + 128:256 * b + 256], A.add))
-        need("Y", y_ok)
-        y_out = done(Y.dma_start(T.y[:, 256 * p:256 * p + 256], T.yb[:, 256 * p:256 * p + 256]), "d_y", 16)
+    def first(q, b):
+        a[b] = move(q, part("acc", b, 0), upick(b, 0, 16), *ub_ok[b])
+
+    def chain(b, s):
+        need("V", a[b], *ub_ok[b])
+        a[b] = dv(V.tensor_tensor(part("acc", b, s), upick(b, 16 * s, 16 * s + 16), part("acc", b, s - 1), A.add))
+
+    def half(q, b):
+        a["h", b] = move(q, T.fin[:, 128 * b:128 * b + 128], part("acc", b, 3).indirect(T.fio[:, 0:8]), a[b], m_fio)
+
+    def close(b):
+        need("V", a["h", b], a[b], m_fio)
+        a["y", b] = dv(V.tensor_tensor(T.yb[:, 128 * b:128 * b + 128], part("acc", b, 3).indirect(T.fio[:, 8:16]),
+                                       T.fin[:, 128 * b:128 * b + 128], A.add))
+
+    def spread(q, b, s, n):
+        a["s", b, s] = move(q, part("acc", b, s, 1024 // n), upick(b, 64 + 64 // n * s, 64 + 64 // n * (s + 1)), *ub_ok[b])
+
+    def scan(b, s, n):
+        need("V", a["s", b, s], m_cs)
+        a["t", b, s] = dv(V.tensor_tensor_scan(part("sum", b, s, 1024 // n), T.cs8[:, 0:1024 // n],
+                                               part("acc", b, s, 1024 // n), 0.0, A.mult, A.add))
+
+    def ends(q, b, n):
+        a["y", b] = move(q, T.yb[:, 128 * b:128 * b + 128], T.sum[:, 1024 * b + 7:1024 * b + 1024:8],
+                         *[a["t", b, s] for s in range(n)])
+
+    def store(lo, hi):
+        need("Y", *[a["y", b] for b in range(lo, hi)])
+        return done(Y.dma_start(T.y[:, 128 * lo:128 * hi], T.yb[:, 128 * lo:128 * hi]), "d_y", 16)
+
+    copy("S", 0); copy("V", 1); first("S", 0); first("V", 1)
+    copy("S", 2); spread("S", 2, 0, 1)
+    for s in (1, 2, 3):
+        chain(0, s); chain(1, s)
+    copy("S", 3); spread("S", 3, 0, 2); half("S", 0); half("S", 1); spread("S", 3, 1, 2)
+    scan(2, 0, 1); close(0); close(1); store(0, 2)
+    scan(3, 0, 2); ends("S", 2, 1); store(2, 3); scan(3, 1, 2); ends("V", 3, 2)
+    y_out = store(3, 4)
     need("Y", y_out)
     need("G", ("ls", cnt["ls"]))

@@ -4,17 +4,24 @@ from concourse.mybir import dt, AluOpType, ActivationFunctionType
 N, NT, CAP = 8, 128, 96
 ALL = N * CAP
 UW = 8 + ALL
-CW = 2 * 7 * CAP + 128
+CW = 32 + 2 * 7 * CAP + 128
 CODES = "float8_e4m3fn_x4"
-CHUNKS = [(1,), (2, 3, 4), (5, 6, 7)]
-HELP_F = (0, 0, 192)
-HELP_B = (0, 0, 96)
-LATE = 3
+GROUPS = {"f": [(0, 1, 2), (3, 4), (5, 6, 7)], "b": [(0, 1, 2), (3, 4), (5, 6, 7)]}
+PLAN = {
+    "f": [((7,), 0, [[("C", 4, 4, [(7, 4, 4)])], [("S", 0, 4, [(7, 0, 4)])]]),
+          ((1, 2), 0, [[("c", 1, 0, 4), ("c", 2, 4, 4)], [("s", 1, 0, 4), ("s", 2, 4, 4)]]),
+          ((3, 4), 96, [[("c", 3, 0, 4), ("c", 4, 4, 4)], [("s", 3, 0, 4), ("s", 4, 4, 4)]]),
+          ((5, 6), 96, [[("c", 5, 0, 4), ("c", 6, 4, 4)], [("s", 5, 0, 4), ("s", 6, 4, 4)]])],
+    "b": [((1, 2), 0, [[("S", 0, 8, [(1, 0, 4), (2, 4, 4)])], [("c", 1, 0, 4), ("c", 2, 4, 4)]]),
+          ((3, 4), 0, [[("c", 3, 0, 4), ("c", 4, 4, 4), ("S", 0, 8, [(3, 0, 4), (4, 4, 4)])]]),
+          ((5, 6, 7), 96, [[("c", 5, 0, 4), ("c", 6, 4, 2), ("c", 7, 6, 2), ("S", 0, 8, [(5, 0, 4), (6, 4, 4)])],
+                           [("s", 7, 0, 4)]])],
+}
 
 SCRATCH = {
     "xb": ("sbuf", [128, 528], "bfloat16"),
     "snw": ("sbuf", [128, 48], "int32"), "snof": ("sbuf", [128, 192], "uint16"),
-    "xt": ("sbuf", [128, 4 * ALL], "bfloat16"),
+    "xt": ("sbuf", [128, 4 * (32 + ALL)], "bfloat16"),
     "cf": ("sbuf", [128, CW], CODES), "sf": ("sbuf", [128, CW], "uint8"),
     "cb": ("sbuf", [128, CW], CODES), "sb": ("sbuf", [128, CW], "uint8"),
     "wb": ("sbuf", [128, 2048], "bfloat16"), "wq": ("sbuf", [128, 512], CODES), "ws": ("sbuf", [128, 512], "uint8"),
@@ -26,7 +33,8 @@ SCRATCH = {
     "pa": ("sbuf", [128, 8], "int32"), "pb": ("sbuf", [128, 8], "int32"), "pc": ("sbuf", [128, 8], "int32"),
     "pd": ("sbuf", [128, 8], "int32"), "pof": ("sbuf", [128, 8], "uint16"),
     "iv1": ("sbuf", [128, 128], "float32"), "iv2": ("sbuf", [128, 128], "float32"), "ivv": ("sbuf", [128, 128], "float32"),
-    "inv": ("sbuf", [128, ALL], "float32"), "invw": ("sbuf", [128, 48], "float32"), "ivo": ("sbuf", [128, 48], "uint16"),
+    "inv": ("sbuf", [128, ALL], "float32"), "invw": ("sbuf", [128, 96], "float32"), "invs": ("sbuf", [128, 48], "float32"),
+    "ivo": ("sbuf", [128, 48], "uint16"),
     "pi": ("sbuf", [128, 1], "int32"), "k15": ("sbuf", [128, 1], "int32"), "k3": ("sbuf", [128, 1], "int32"),
     "k12": ("sbuf", [128, 1], "int32"), "f8": ("sbuf", [128, 1], "float32"), "f12": ("sbuf", [128, 1], "float32"),
     "fgr": ("sbuf", [128, 1], "float32"),
@@ -34,7 +42,6 @@ SCRATCH = {
     "fipat": ("sbuf", [128, 16], "int32"), "fio": ("sbuf", [128, 16], "uint16"),
     "grb": ("sbuf", [128, 512], "bfloat16"),
     "z0": ("sbuf", [128, 512], "float32"), "m1": ("sbuf", [128, 512], "float32"), "m2": ("sbuf", [128, 512], "float32"),
-    "zs": ("sbuf", [128, 768], "float32"), "rs": ("sbuf", [128, 768], "float32"), "cm": ("sbuf", [128, 768], "bfloat16"),
     "d0": ("sbuf", [128, 2048], "bfloat16"), "d1": ("sbuf", [128, 1024], "bfloat16"),
     "ca": ("sbuf", [128, 1024], "bfloat16"), "cs8": ("sbuf", [128, 1024], "bfloat16"),
     "gg": ("sbuf", [128, 4096], "bfloat16"),
@@ -45,29 +52,75 @@ SCRATCH = {
     "fin": ("sbuf", [128, 512], "float32"), "yb": ("sbuf", [128, 512], "float32"),
 }
 SEMAPHORES = ["cv", "cs", "ct", "cp", "d_x", "d_sn", "d_w", "d_v", "d_gr", "d_nd", "d_nb", "d_n8", "d_id", "d_il",
-              "d_add", "d_ad2", "d_iv", "d_y", "f0", "f1", "b0", "b1", "ls"]
+              "d_add", "d_iv", "d_y", "f0", "f1", "f2", "b0", "b1", "b2", "hf0", "hf1", "hf2", "hb0", "hb1", "hb2", "hb3", "ls"]
 
 
 def way(ph, s, j):
     if ph == "f":
-        return (s - j) % N, CAP * (7 - j), 7 * CAP + 128 + CAP * (j - 1)
+        return (s - j) % N, 32 + CAP * (7 - j), 32 + 7 * CAP + 128 + CAP * (j - 1)
     return (s + j) % N, 7 * CAP + 128 + CAP * (j - 1), CAP * (7 - j)
 
 
-def shares(n, flip):
-    s = {1: [8], 2: [4, 4], 3: [4, 2, 2], 4: [2, 2, 2, 2]}[n]
-    return s[::-1] if flip else s
+def group_of(ph, j):
+    return [j in steps for steps in GROUPS[ph]].index(True)
 
 
-def group_of(j):
-    return 1 if j > 7 - LATE else 0
+def helper_of(s, cores, topo):
+    c = cores[s]
+    return [h for h in topo.cores_of(c) if h != c and topo.die(h) != topo.die(c)
+            and all(topo.may_write(h, d) for d in cores)][0]
+
+
+def hands(ph):
+    out = []
+    for _, _, calls in PLAN[ph]:
+        for call in calls:
+            for item in call:
+                if item[0] in "CS":
+                    lo, n = min(way(ph, 0, j)[1] for j, _, _ in item[3]), CAP * len(item[3])
+                    if item[0] == "S" and len(call) > 1:
+                        lo, n = (lo if ph == "f" else lo + n - 4 * CAP), 4 * CAP
+                    out.append((item, lo, n, sum(x[2] for x in out if x[0][0] == item[0])))
+    return out
+
+
+def arrivals(ph, grp):
+    items = [item for _, _, calls in PLAN[ph] for call in calls for item in call]
+    return (sum(item[3] for item in items if item[0] in "cs" and group_of(ph, item[1]) == grp)
+            + sum(n for item in items if item[0] in "CS" for j, _, n in item[3] if group_of(ph, j) == grp))
+
+
+def block(T, topo, me, s, ph, j, buf, at, first, n):
+    d, _, b = way(ph, s, j)
+    rid, pid, _ = topo.addr(T.cores[d])
+    x, y = T[buf][:, at:at + CAP], T[buf][:, b:b + CAP]
+    if buf[0] == "c":
+        x, y = x.bitcast(dt.uint8), y.bitcast(dt.uint8)
+    return RemoteDMATransfer(dst_ids=[DstId(rid=rid, pnc=pid)],
+                             dma_engine_mask=sum(1 << e for e in topo.engines(me, T.cores[d])[first:first + n]),
+                             remote_sem=T.sem[ph + str(group_of(ph, j))], srcs=[x], dsts=[y])
+
+
+def helper_program(g, core, s, T, topo):
+    left = 0
+    for ph in "fb":
+        for i, (item, lo, _, at) in sorted(enumerate(hands(ph)), key=lambda x: x[1][0][0] == "C"):
+            g.wait_ge(T.sem["h" + ph + str(i)], item[2])
+            g.remote_dma_fused([block(T, topo, core, s, ph, j, item[0].lower() + ph, way(ph, s, j)[1] - lo + at, e, n)
+                                for j, e, n in item[3]], local_sem=T.sem["ls"])
+            left += sum(n for _, _, n in item[3])
+    if left:
+        g.wait_ge(T.sem["ls"], left)
 
 
 def rank_program(g, core, T, topo):
     r = T.rank_of(core)
-    if r is None:
-        return
     cores = list(T.cores)
+    if r is None:
+        for s in range(N):
+            if helper_of(s, cores, topo) == core:
+                helper_program(g, core, s, T, topo)
+        return
     A, COPY = AluOpType, ActivationFunctionType.Copy
     V, S, P, Y = g.vector, g.scalar, g.tensor, g.sync
     qn = {"V": V, "S": S, "P": P, "Y": Y, "G": g}
@@ -117,33 +170,38 @@ def rank_program(g, core, T, topo):
         nb_in = done(Y.dma_start(T.nbw[16 * k:16 * k + 16, :], T.nbd[:, :]), "d_nb", 16)
 
     m_pi = dg(g.iota(T.pi[:, :], [[0, 1]], 0, 1))
-    m_grp = dg(g.iota(T.grpat[:, :], [[2, 2], [16, 8], [1, 2]], 0, 0))
     iota(T.iv1[:, :], [[128, 8], [-2, 2], [0, 8]], 3, 1)
     m_iv = iota(T.iv2[:, :], [[0, 16], [1024, 2], [4, 4]])
+    m_grp = dg(g.iota(T.grpat[:, :], [[2, 2], [16, 8], [1, 2]], 0, 0))
 
     m_pad = dv(V.memset(T.xb[:, 0:16], 0.0))
     m_inv = dv(V.memset(T.inv[:, :], 0.0))
     m_d1 = dv(V.memset(T.d1[:, :], 0.0))
 
-    arrived = {}
+    arrived = {ph: [(ph + str(grp), arrivals(ph, grp)) for grp in range(len(GROUPS[ph]))] for ph in "fb"}
+    helper = helper_of(r, cores, topo)
+    near = [e for e in topo.engines(core, helper) if e not in topo.engines(core, cores[r - 1])]
 
-    def send(ph, codes, planes, i):
-        for buf in (codes, planes):
-            tr, k = [], 0
-            for j, n in zip(CHUNKS[i], shares(len(CHUNKS[i]), (buf is planes) != (i % 2 == 0))):
-                d, a, b = way(ph, r, j)
-                rid, pid, _ = topo.addr(cores[d])
-                x, y = buf[:, a:a + CAP], buf[:, b:b + CAP]
-                if buf is codes:
-                    x, y = x.bitcast(dt.uint8), y.bitcast(dt.uint8)
-                sem = ph + str(group_of(j))
-                tr.append(RemoteDMATransfer(dst_ids=[DstId(rid=rid, pnc=pid)],
-                                            dma_engine_mask=sum(1 << e for e in topo.engines(core, cores[d])[k:k + n]),
-                                            remote_sem=T.sem[sem], srcs=[x], dsts=[y]))
-                k += n
-                arrived[sem] = (sem, arrived.get(sem, (sem, 0))[1] + n)
+    def send(ph, calls):
+        for call in calls:
+            tr = []
+            for item in call:
+                if item[0] in "CS":
+                    i = [x[0] for x in hands(ph)].index(item)
+                    _, lo, n, at = hands(ph)[i]
+                    rid, pid, _ = topo.addr(helper)
+                    buf = T[item[0].lower() + ph]
+                    x, y = buf[:, lo:lo + n], buf[:, at:at + n]
+                    if item[0] == "C":
+                        x, y = x.bitcast(dt.uint8), y.bitcast(dt.uint8)
+                    tr.append(RemoteDMATransfer(dst_ids=[DstId(rid=rid, pnc=pid)],
+                                                dma_engine_mask=sum(1 << e for e in near[item[1]:item[1] + item[2]]),
+                                                remote_sem=T.sem["h" + ph + str(i)], srcs=[x], dsts=[y]))
+                    cnt["ls"] = cnt.get("ls", 0) + item[2]
+                else:
+                    tr.append(block(T, topo, core, r, ph, item[1], item[0] + ph, way(ph, r, item[1])[1], item[2], item[3]))
+                    cnt["ls"] = cnt.get("ls", 0) + item[3]
             g.remote_dma_fused(tr, local_sem=T.sem["ls"])
-            cnt["ls"] = cnt.get("ls", 0) + k
 
     need("V", sn_in)
     snof = [dv(V.tensor_scalar(T.snof[:, 48 * t:48 * t + 48], T.snw[:, :], 4, 16 + t, A.mult, A.add)) for t in range(4)]
@@ -155,7 +213,7 @@ def rank_program(g, core, T, topo):
             for a, b in ((lo, min(hi, turn)), (max(lo, turn), hi)):
                 if a < b and who[t] != ".":
                     e = 48 * t + (a + CAP * (r + 1)) % ALL // 16
-                    marks.append(move(who[t], T.xt[:, 4 * a + t:4 * b:4],
+                    marks.append(move(who[t], T.xt[:, 4 * (32 + a) + t:4 * (32 + b):4],
                                       T.xb[:, 0:528].indirect(T.snof[:, e:e + (b - a) // 16]), x_in, m_pad, snof[t]))
         return marks
 
@@ -163,26 +221,22 @@ def rank_program(g, core, T, topo):
         need("V", *marks)
         return dv(V.quantize_mx(codes[:, at:at + hi - lo], planes[:, at:at + hi - lo], tile[:, 4 * lo:4 * hi]))
 
-    spare = max(0, 128 - CAP * len(CHUNKS[0]))
-    below, above = (spare, 0) if turn == 7 * CAP else (0, spare)
+    below, above = (32, 0) if turn == CAP else (0, 32)
     f_q = []
-    for i, steps in enumerate(CHUNKS):
+    for i, (steps, over, calls) in enumerate(PLAN["f"]):
         lo, hi = CAP * (7 - steps[-1]), CAP * (8 - steps[0])
         if i == 0:
             lo, hi = lo - below, hi + above
-        top = hi - (below if i == 1 else 0)
-        if HELP_F[i]:
-            marks = pick_x("SS.V", lo, top) + pick_x("..V.", lo, top - HELP_F[i]) + pick_x("..S.", top - HELP_F[i], top)
+        low = lo + (above if lo == CAP else 0)
+        if over:
+            marks = pick_x("SS.V", low, hi) + pick_x("..V.", low, hi - over) + pick_x("..S.", hi - over, hi)
         else:
-            marks = pick_x("SSVV", lo, top)
-        f_q = [quantise(T.cf, T.sf, lo, T.xt, lo, hi, marks + (f_q if below else []))]
+            marks = pick_x("SSVV", low, hi)
+        f_q = [quantise(T.cf, T.sf, 32 + lo, T.xt, 32 + lo, 32 + hi, marks + (f_q if lo == CAP else []))]
         need("G", *f_q)
-        send("f", T.cf, T.sf, i)
-    own = pick_x("SSSS", 7 * CAP + above, ALL)
+        send("f", calls)
+    own = pick_x("SSSS", 7 * CAP, ALL)
 
-    need("V", w_in)
-    w_q = dv(V.quantize_mx(T.wq[:, 0:512], T.ws[:, 0:512], T.wb[:, 0:2048]))
-    own_f = quantise(T.cf, T.sf, 7 * CAP, T.xt, ALL - 128, ALL, own + f_q)
     need("V", n8_in, m_pi)
     p_a = dv(V.tensor_scalar(T.pa[:, :], T.nb8[:, :], 15, None, A.bitwise_and))
     p_b = dv(V.tensor_scalar(T.pb[:, :], T.nb8[:, :], 4, None, A.arith_shift_right))
@@ -193,31 +247,31 @@ def rank_program(g, core, T, topo):
     m_ivv = dv(V.tensor_tensor(T.ivv[:, :], T.iv1[:, :], T.iv2[:, :], A.add))
     need("V", p_c, p_b)
     p_d = dv(V.tensor_tensor(T.pd[:, :], T.pc[:, :], T.pb[:, :], A.add))
-    need("V", nb_in)
-    for bl in range(2):
-        m_zo = dv(V.tensor_scalar(T.zof[:, bl:64:2], T.nbw[:, :], ALL * bl, None, A.add))
+    k3 = dv(V.tensor_scalar(T.k3[:, :], T.pi[:, :], 3, None, A.bitwise_and))
     need("V", p_d)
     p_of = dv(V.tensor_copy(T.pof[:, :], T.pd[:, :]))
-    k3 = dv(V.tensor_scalar(T.k3[:, :], T.pi[:, :], 3, None, A.bitwise_and))
     need("V", k12)
     m_f12 = dv(V.tensor_copy(T.f12[:, :], T.k12[:, :]))
     need("V", p_of, m_inv, m_ivv)
     m_sc = dv(V.tensor_copy(T.inv[:, 0:ALL].indirect(T.pof[:, 0:8]), T.ivv[:, :]))
+    need("V", w_in)
+    w_q = dv(V.quantize_mx(T.wq[:, 0:512], T.ws[:, 0:512], T.wb[:, 0:2048]))
+    own_f = quantise(T.cf, T.sf, 32 + 7 * CAP, T.xt, 32 + ALL - 128, 32 + ALL, own + f_q)
     need("V", m_f12, k3)
     m_fgr = dv(V.tensor_scalar(T.fgr[:, :], T.k3[:, :], 128, T.f12[:, :], A.mult, A.add))
-    m_cm = [dv(V.memset(T.cm[:, k:768:3], 0.0 if k else -1e29)) for k in range(3)]
+    need("V", nb_in)
+    for bl in range(2):
+        m_zo = dv(V.tensor_scalar(T.zof[:, bl:64:2], T.nbw[:, :], ALL * bl, None, A.add))
     need("V", m_fgr, m_grp)
     m_gro = dv(V.tensor_scalar(T.gro[:, :], T.grpat[:, :], T.fgr[:, :], None, A.add))
+    m_d0 = dv(V.memset(T.d0[:, 0:2048:4], 0.0))
 
     def lay_gr(p, *marks):
         return move("S", T.d1[:, 0:1024:4], T.grb[:, 0:512].indirect(T.gro[:, 16 * p:16 * p + 16]), m_gro, gr_in, *marks)
 
     need("G", m_sc)
     done(g.dma_start(T.inv[0:1, :], T.inv[32:33, :], accum_op=A.add), "d_add", 16)
-    add = done(g.dma_start(T.inv[16:17, :], T.inv[48:49, :], accum_op=A.add), "d_add", 16)
-    m_d0 = iota(T.d0[:, 0:2048:4], [[0, 512]])
-    need("G", add)
-    added = done(g.dma_start(T.inv[0:1, :], T.inv[16:17, :], accum_op=A.add), "d_ad2", 16)
+    added = done(g.dma_start(T.inv[16:17, :], T.inv[48:49, :], accum_op=A.add), "d_add", 16)
     m_ca = iota(T.ca[:, :], [[0, 512], [-1, 2]])
     for b in range(4):
         m_up = iota(T.ub[:, UW * b:UW * b + 8], [[0, 8]])
@@ -226,41 +280,50 @@ def rank_program(g, core, T, topo):
     need("G", m_c1)
     m_cs = iota(T.cs8[:, 0:1024:8], [[0, 128]])
 
-    need("Y", arrived["f1"])
-    v_in = done(Y.dma_start(T.vb[:, :], T.w2[:, :]), "d_v", 16)
+    need("Y", added)
+    for k in range(8):
+        for e in range(2):
+            iv_in = done(Y.dma_start(T.invw[16 * k:16 * k + 16, 48 * e:48 * e + 48], T.inv[16 * e:16 * e + 1, :]), "d_iv", 16)
     for s in range(4):
         done(Y.dma_start(T.ild[:, 16 * s:16 * s + 16], T.il[s:16:4, :]), "d_id", 16)
     id_in = done(Y.dma_start(T.ild[:, 64:128], T.il[:, :]), "d_id", 16)
-    need("Y", added)
-    for k in range(8):
-        iv_in = done(Y.dma_start(T.invw[16 * k:16 * k + 16, :], T.inv[0:1, :]), "d_iv", 16)
+    need("Y", arrived["f"][-1])
+    v_in = done(Y.dma_start(T.vb[:, :], T.w2[:, :]), "d_v", 16)
     need("Y", id_in)
     for k in range(8):
         il_in = done(Y.dma_start(T.ilw[16 * k:16 * k + 16, :], T.ild[:, :]), "d_il", 16)
 
     zp_free = {}
 
-    def products(grp, codes, planes, lo, first, n, st, sts, ready, land, wide, pad):
-        need("P", *ready)
+    def products(ph, grp, st, sts, land, wide, pad, *ready):
+        steps, bank = GROUPS[ph][grp], len(zp_free.setdefault("turns", [])) % 2
+        zp_free["turns"].append(grp)
+        n = len(steps)
+        if ph == "f":
+            lo, first = 32 + 7 * CAP + 32 + CAP * steps[0], r + steps[0]
+        else:
+            lo, first = CAP * (7 - steps[-1]), r - steps[-1]
+        need("P", arrived[ph][grp], *ready)
         mm = []
         for b in range(4):
-            at = 512 * (2 * b + grp)
-            need("P", *zp_free.get((b, grp), []))
+            at = 512 * (2 * b + bank)
+            need("P", *zp_free.get((b, bank), []))
             mm.append(done(P.matmul_mx(T.zp[:, at:at + CAP * n], st[:, 128 * b:128 * b + 128], sts[:, 128 * b:128 * b + 128],
-                                       codes[:, lo:lo + CAP * n], planes[:, lo:lo + CAP * n], True, True), "ct"))
+                                       T["c" + ph][:, lo:lo + CAP * n], T["s" + ph][:, lo:lo + CAP * n], True, True), "ct"))
 
         def take(q, b):
-            at, to = 512 * (2 * b + grp), wide * b + pad
-            zp_free[(b, grp)] = [move(q, land[:, to + CAP * d:to + CAP * (d + k)], T.zp[:, at + CAP * o:at + CAP * (o + k)],
-                                      mm[b]) for o, d, k in runs(first, n)]
-            return zp_free[(b, grp)]
+            at, to = 512 * (2 * b + bank), wide * b + pad
+            zp_free[(b, bank)] = [move(q, land[:, to + CAP * d:to + CAP * (d + k)], T.zp[:, at + CAP * o:at + CAP * (o + k)],
+                                       mm[b]) for o, d, k in runs(first, n)]
+            return zp_free[(b, bank)]
         return take
 
     zb_ok = {b: [] for b in range(4)}
-    take = products(0, T.cf, T.sf, 7 * CAP + 32, r, N - LATE, T.wq, T.ws, (w_q, own_f, arrived["f0"]), T.zb, ALL, 0)
-    for q, b in zip("SSVS", range(4)):
-        zb_ok[b] += take(q, b)
-    take = products(1, T.cf, T.sf, CW - CAP * LATE, r - LATE, LATE, T.wq, T.ws, (arrived["f1"],), T.zb, ALL, 0)
+    for grp in range(len(GROUPS["f"])):
+        take = products("f", grp, T.wq, T.ws, T.zb, ALL, 0, w_q, own_f)
+        if grp < len(GROUPS["f"]) - 1:
+            for q, b in zip("SVSV", range(4)):
+                zb_ok[b] += take(q, b)
     zb_ok[0] += take("S", 0)
     zb_ok[1] += take("V", 1)
 
@@ -276,11 +339,7 @@ def rank_program(g, core, T, topo):
     zb_ok[2] += take("S", 2)
     zb_ok[3] += take("S", 3)
     d1_ok = {0: lay_gr(0, m_d1)}
-    c["zs"] = [move("S", T.zs[:, k:768:3], zpick(1, k), *zb_ok[2], *zb_ok[3]) for k in range(3)]
-
-    def running():
-        need("V", *c["zs"], *m_cm)
-        c["rs"] = dv(V.tensor_tensor_scan(T.rs[:, :], T.cm[:, :], T.zs[:, :], 0.0, A.add, A.max))
+    c["z0", 1] = [move("S", seg("z0", 1), zpick(1, 0), *zb_ok[2], *zb_ok[3])]
 
     def vmax(p, k):
         src, dst = (("z0", "m1"), ("m1", "m2"))[k - 1]
@@ -289,9 +348,8 @@ def rank_program(g, core, T, topo):
 
     def vrec(p, k):
         src = ("z0", "m1", "m2")[k - 1]
-        need("V", *(c[src, p] if p == 0 else [c["rs"]]))
-        c["n", p, k] = dv(V.tensor_tensor(T.d0[:, 1024 * p + 4 - k:1024 * p + 1024:4], zpick(p, k),
-                                          seg(src, p) if p == 0 else T.rs[:, k - 1:768:3], A.is_le))
+        need("V", *c[src, p])
+        c["n", p, k] = dv(V.tensor_tensor(T.d0[:, 1024 * p + 4 - k:1024 * p + 1024:4], zpick(p, k), seg(src, p), A.is_le))
 
     def keep(p):
         need("V", m_d0, d1_ok[p], *[c["n", p, k] for k in (1, 2, 3)])
@@ -314,20 +372,22 @@ def rank_program(g, core, T, topo):
                     T.gg[:, 2048 * p + 64 * bl:2048 * p + 2048].indirect(T.ivo[:, lo // 16:hi // 16]), c["g", p], *iv_ok)
 
     vmax(0, 1); vrec(0, 1); vmax(0, 2); vrec(0, 2); vrec(0, 3)
-    keep(0); running(); odd(0)
+    vmax(1, 1); keep(0); vrec(1, 1); odd(0)
     d1_ok[1] = lay_gr(1, c["k", 0])
     need("V", iv_in)
-    iv_ok = [dv(V.tensor_copy(T.ivo[:, 6 * o:6 * (o + k)], T.invw[:, 6 * d:6 * (d + k)])) for o, d, k in runs(r, N)]
+    iv_sum = dv(V.tensor_tensor(T.invs[:, :], T.invw[:, 0:48], T.invw[:, 48:96], A.add))
     second(0)
+    need("V", iv_sum)
+    iv_ok = [dv(V.tensor_copy(T.ivo[:, 6 * o:6 * (o + k)], T.invs[:, 6 * d:6 * (d + k)])) for o, d, k in runs(r, N)]
     h_ok = [place("S", 0, 0, ALL), place("S", 1, 0, ALL)]
-    vrec(1, 1); vrec(1, 2); vrec(1, 3); keep(1); odd(1); second(1)
-    for i, steps in enumerate(CHUNKS):
+    vmax(1, 2); vrec(1, 2); vrec(1, 3); keep(1); odd(1); second(1)
+    spare = max(0, 128 - CAP * len(PLAN["b"][0][0]))
+    for i, (steps, over, calls) in enumerate(PLAN["b"]):
         lo, hi = CAP * steps[0] - (spare if i == 0 else 0), CAP * (steps[-1] + 1)
-        cut = hi - HELP_B[i]
-        marks = [place("S", 2, lo, hi), place("V", 3, lo, cut)] + ([place("S", 3, cut, hi)] if cut < hi else [])
+        marks = [place("S", 2, lo, hi), place("V", 3, lo, hi - over)] + ([place("S", 3, hi - over, hi)] if over else [])
         b_q = quantise(T.cb, T.sb, 7 * CAP + 32 + lo, T.h, lo, hi, marks + h_ok)
         need("G", b_q)
-        send("b", T.cb, T.sb, i)
+        send("b", calls)
     own = [place("S", 2, 0, CAP - spare), place("S", 3, 0, CAP - spare)]
 
     need("V", v_in)
@@ -342,10 +402,11 @@ def rank_program(g, core, T, topo):
     m_fio = dv(V.tensor_scalar(T.fio[:, :], T.fipat[:, :], T.f8[:, :], None, A.add))
 
     ub_ok = {b: [m_iq, m_up] for b in range(4)}
-    take = products(0, T.cb, T.sb, CAP * LATE, r + 1 + LATE, N - LATE, T.vq, T.vs, (v_q, own_b, arrived["b0"]), T.ub, UW, 8)
-    for q, b in zip("SVSV", range(4)):
-        ub_ok[b] += take(q, b)
-    take = products(1, T.cb, T.sb, 0, r + 1, LATE, T.vq, T.vs, (arrived["b1"],), T.ub, UW, 8)
+    for grp in range(len(GROUPS["b"])):
+        take = products("b", grp, T.vq, T.vs, T.ub, UW, 8, v_q, own_b)
+        if grp < len(GROUPS["b"]) - 1:
+            for q, b in zip("SVSV", range(4)):
+                ub_ok[b] += take(q, b)
 
     def upick(b, lo, hi):
         return T.ub[:, UW * b:UW * b + UW].indirect(T.ilq[:, lo:hi])

from concourse.bass import DstId, RemoteDMATransfer
from concourse.mybir import dt, AluOpType, ActivationFunctionType

N, NT, CAP = 8, 128, 96
ALL = N * CAP
UW = 8 + ALL
CW = 32 + 2 * 7 * CAP + 128
CODES = "float8_e4m3fn_x4"
GROUPS = {"f": [(0, 1, 2), (3, 4), (5, 6, 7)], "b": [(0, 1, 2), (3, 4), (5, 6, 7)]}
PLAN = {
    "f": [((7,), 0, [[("C", 4, 4, [(7, 4, 4)])], [("S", 0, 4, [(7, 0, 4)])]]),
          ((1, 2), 0, [[("c", 1, 0, 4), ("c", 2, 4, 4)], [("s", 1, 0, 4), ("s", 2, 4, 4)]]),
          ((3, 4), 96, [[("c", 3, 0, 4), ("c", 4, 4, 4)], [("s", 3, 0, 4), ("s", 4, 4, 4)]]),
          ((5, 6), 96, [[("c", 5, 0, 4), ("c", 6, 4, 4)], [("s", 5, 0, 4), ("s", 6, 4, 4)]])],
    "b": [((1, 2), 0, [[("S", 0, 8, [(1, 0, 4), (2, 4, 4)])], [("c", 1, 0, 4), ("c", 2, 4, 4)]]),
          ((3, 4), 0, [[("c", 3, 0, 4), ("c", 4, 4, 4), ("S", 0, 8, [(3, 0, 4), (4, 4, 4)])]]),
          ((5, 6, 7), 96, [[("c", 5, 0, 4), ("c", 6, 4, 2), ("c", 7, 6, 2), ("S", 0, 8, [(5, 0, 4), (6, 4, 4)])],
                           [("s", 7, 0, 4)]])],
}

SCRATCH = {
    "xb": ("sbuf", [128, 528], "bfloat16"),
    "snw": ("sbuf", [128, 48], "int32"), "snof": ("sbuf", [128, 192], "uint16"),
    "xt": ("sbuf", [128, 4 * (32 + ALL)], "bfloat16"),
    "cf": ("sbuf", [128, CW], CODES), "sf": ("sbuf", [128, CW], "uint8"),
    "cb": ("sbuf", [128, CW], CODES), "sb": ("sbuf", [128, CW], "uint8"),
    "wb": ("sbuf", [128, 2048], "bfloat16"), "wq": ("sbuf", [128, 512], CODES), "ws": ("sbuf", [128, 512], "uint8"),
    "vb": ("sbuf", [128, 2048], "bfloat16"), "vq": ("sbuf", [128, 512], CODES), "vs": ("sbuf", [128, 512], "uint8"),
    "zp": ("psum", [128, 4096], "float32"),
    "zb": ("sbuf", [128, 4 * ALL], "float32"),
    "nbd": ("dram", [16, 32], "int32"), "nbw": ("sbuf", [128, 32], "int32"), "zof": ("sbuf", [128, 64], "uint16"),
    "nb8": ("sbuf", [128, 8], "int32"),
    "pa": ("sbuf", [128, 8], "int32"), "pb": ("sbuf", [128, 8], "int32"), "pc": ("sbuf", [128, 8], "int32"),
    "pd": ("sbuf", [128, 8], "int32"), "pof": ("sbuf", [128, 8], "uint16"),
    "iv1": ("sbuf", [128, 128], "float32"), "iv2": ("sbuf", [128, 128], "float32"), "ivv": ("sbuf", [128, 128], "float32"),
    "inv": ("sbuf", [128, ALL], "float32"), "invw": ("sbuf", [128, 96], "float32"), "invs": ("sbuf", [128, 48], "float32"),
    "ivo": ("sbuf", [128, 48], "uint16"),
    "pi": ("sbuf", [128, 1], "int32"), "k15": ("sbuf", [128, 1], "int32"), "k3": ("sbuf", [128, 1], "int32"),
    "k12": ("sbuf", [128, 1], "int32"), "f8": ("sbuf", [128, 1], "float32"), "f12": ("sbuf", [128, 1], "float32"),
    "fgr": ("sbuf", [128, 1], "float32"),
    "grpat": ("sbuf", [128, 32], "int32"), "gro": ("sbuf", [128, 32], "uint16"),
    "fipat": ("sbuf", [128, 16], "int32"), "fio": ("sbuf", [128, 16], "uint16"),
    "grb": ("sbuf", [128, 512], "bfloat16"),
    "z0": ("sbuf", [128, 512], "float32"), "m1": ("sbuf", [128, 512], "float32"), "m2": ("sbuf", [128, 512], "float32"),
    "d0": ("sbuf", [128, 2048], "bfloat16"), "d1": ("sbuf", [128, 1024], "bfloat16"),
    "ca": ("sbuf", [128, 1024], "bfloat16"), "cs8": ("sbuf", [128, 1024], "bfloat16"),
    "gg": ("sbuf", [128, 4096], "bfloat16"),
    "h": ("sbuf", [128, 4 * ALL], "bfloat16"),
    "ub": ("sbuf", [128, 4 * UW], "float32"),
    "ild": ("dram", [16, 128], "int32"), "ilw": ("sbuf", [128, 128], "int32"), "ilq": ("sbuf", [128, 128], "uint16"),
    "acc": ("sbuf", [128, 4096], "float32"), "sum": ("sbuf", [128, 4096], "float32"),
    "fin": ("sbuf", [128, 512], "float32"), "yb": ("sbuf", [128, 512], "float32"),
}
SEMAPHORES = ["cv", "cs", "ct", "cp", "d_x", "d_sn", "d_w", "d_v", "d_gr", "d_nd", "d_nb", "d_n8", "d_id", "d_il",
              "d_add", "d_iv", "d_y", "f0", "f1", "f2", "b0", "b1", "b2", "hf0", "hf1", "hf2", "hb0", "hb1", "hb2", "hb3", "ls"]


def way(ph, s, j):
    if ph == "f":
        return (s - j) % N, 32 + CAP * (7 - j), 32 + 7 * CAP + 128 + CAP * (j - 1)
    return (s + j) % N, 7 * CAP + 128 + CAP * (j - 1), CAP * (7 - j)


def group_of(ph, j):
    return [j in steps for steps in GROUPS[ph]].index(True)


def helper_of(s, cores, topo):
    c = cores[s]
    return [h for h in topo.cores_of(c) if h != c and topo.die(h) != topo.die(c)
            and all(topo.may_write(h, d) for d in cores)][0]


def hands(ph):
    out = []
    for _, _, calls in PLAN[ph]:
        for call in calls:
            for item in call:
                if item[0] in "CS":
                    lo, n = min(way(ph, 0, j)[1] for j, _, _ in item[3]), CAP * len(item[3])
                    if item[0] == "S" and len(call) > 1:
                        lo, n = (lo if ph == "f" else lo + n - 4 * CAP), 4 * CAP
                    out.append((item, lo, n, sum(x[2] for x in out if x[0][0] == item[0])))
    return out


def arrivals(ph, grp):
    items = [item for _, _, calls in PLAN[ph] for call in calls for item in call]
    return (sum(item[3] for item in items if item[0] in "cs" and group_of(ph, item[1]) == grp)
            + sum(n for item in items if item[0] in "CS" for j, _, n in item[3] if group_of(ph, j) == grp))


def block(T, topo, me, s, ph, j, buf, at, first, n):
    d, _, b = way(ph, s, j)
    rid, pid, _ = topo.addr(T.cores[d])
    x, y = T[buf][:, at:at + CAP], T[buf][:, b:b + CAP]
    if buf[0] == "c":
        x, y = x.bitcast(dt.uint8), y.bitcast(dt.uint8)
    return RemoteDMATransfer(dst_ids=[DstId(rid=rid, pnc=pid)],
                             dma_engine_mask=sum(1 << e for e in topo.engines(me, T.cores[d])[first:first + n]),
                             remote_sem=T.sem[ph + str(group_of(ph, j))], srcs=[x], dsts=[y])


def helper_program(g, core, s, T, topo):
    left = 0
    for ph in "fb":
        for i, (item, lo, _, at) in sorted(enumerate(hands(ph)), key=lambda x: x[1][0][0] == "C"):
            g.wait_ge(T.sem["h" + ph + str(i)], item[2])
            g.remote_dma_fused([block(T, topo, core, s, ph, j, item[0].lower() + ph, way(ph, s, j)[1] - lo + at, e, n)
                                for j, e, n in item[3]], local_sem=T.sem["ls"])
            left += sum(n for _, _, n in item[3])
    if left:
        g.wait_ge(T.sem["ls"], left)


def rank_program(g, core, T, topo):
    r = T.rank_of(core)
    cores = list(T.cores)
    if r is None:
        for s in range(N):
            if helper_of(s, cores, topo) == core:
                helper_program(g, core, s, T, topo)
        return
    A, COPY = AluOpType, ActivationFunctionType.Copy
    V, S, P, Y = g.vector, g.scalar, g.tensor, g.sync
    qn = {"V": V, "S": S, "P": P, "Y": Y, "G": g}
    cnt, seen = {}, {}

    def done(ins, sem, n=1):
        ins.then_inc(T.sem[sem], n)
        cnt[sem] = cnt.get(sem, 0) + n
        return (sem, cnt[sem])

    def need(q, *marks):
        best = {}
        for m in marks:
            best[m[0]] = max(best.get(m[0], 0), m[1])
        for sem, val in best.items():
            if seen.get((q, sem), 0) < val:
                qn[q].wait_ge(T.sem[sem], val)
                seen[(q, sem)] = val

    def dv(ins): return done(ins, "cv")
    def ds(ins): return done(ins, "cs")
    def dg(ins): return done(ins, "cp")

    def move(q, out, src, *marks):
        need(q, *marks)
        return ds(S.activation(out, src, COPY)) if q == "S" else dv(V.tensor_copy(out, src))

    def runs(first, n):
        first %= N
        k = min(n, N - first)
        return [(0, first, k)] + ([(k, 0, n - k)] if k < n else [])

    def iota(out, pattern, base=0, step=0):
        return dg(g.iota(out, pattern, base, step, allow_small_or_imprecise_dtypes=True))

    x_in = done(S.dma_start(T.xb[:, 16:528], T.x[:, :]), "d_x", 16)
    for k in range(8):
        sn_in = done((Y if k < 5 else S).dma_start(T.snw[16 * k:16 * k + 16, :], T.sn[:, :]), "d_sn", 16)
    for k in range(4):
        nd_in = done(Y.dma_start(T.nbd[:, 8 * k:8 * k + 8], T.nb[k:16:4, :]), "d_nd", 16)
    for k in range(2):
        n8_in = done(S.dma_start(T.nb8[64 * k:64 * k + 64, :], T.nb[:, :]), "d_n8", 16)
    w_in = done(Y.dma_start(T.wb[:, :], T.w[:, :]), "d_w", 16)
    gr_in = done(S.dma_start(T.grb[:, :], T.gr[:, :]), "d_gr", 16)
    need("Y", nd_in)
    for k in range(8):
        nb_in = done(Y.dma_start(T.nbw[16 * k:16 * k + 16, :], T.nbd[:, :]), "d_nb", 16)

    m_pi = dg(g.iota(T.pi[:, :], [[0, 1]], 0, 1))
    iota(T.iv1[:, :], [[128, 8], [-2, 2], [0, 8]], 3, 1)
    m_iv = iota(T.iv2[:, :], [[0, 16], [1024, 2], [4, 4]])
    m_grp = dg(g.iota(T.grpat[:, :], [[2, 2], [16, 8], [1, 2]], 0, 0))

    m_pad = dv(V.memset(T.xb[:, 0:16], 0.0))
    m_inv = dv(V.memset(T.inv[:, :], 0.0))
    m_d1 = dv(V.memset(T.d1[:, :], 0.0))

    arrived = {ph: [(ph + str(grp), arrivals(ph, grp)) for grp in range(len(GROUPS[ph]))] for ph in "fb"}
    helper = helper_of(r, cores, topo)
    near = [e for e in topo.engines(core, helper) if e not in topo.engines(core, cores[r - 1])]

    def send(ph, calls):
        for call in calls:
            tr = []
            for item in call:
                if item[0] in "CS":
                    i = [x[0] for x in hands(ph)].index(item)
                    _, lo, n, at = hands(ph)[i]
                    rid, pid, _ = topo.addr(helper)
                    buf = T[item[0].lower() + ph]
                    x, y = buf[:, lo:lo + n], buf[:, at:at + n]
                    if item[0] == "C":
                        x, y = x.bitcast(dt.uint8), y.bitcast(dt.uint8)
                    tr.append(RemoteDMATransfer(dst_ids=[DstId(rid=rid, pnc=pid)],
                                                dma_engine_mask=sum(1 << e for e in near[item[1]:item[1] + item[2]]),
                                                remote_sem=T.sem["h" + ph + str(i)], srcs=[x], dsts=[y]))
                    cnt["ls"] = cnt.get("ls", 0) + item[2]
                else:
                    tr.append(block(T, topo, core, r, ph, item[1], item[0] + ph, way(ph, r, item[1])[1], item[2], item[3]))
                    cnt["ls"] = cnt.get("ls", 0) + item[3]
            g.remote_dma_fused(tr, local_sem=T.sem["ls"])

    need("V", sn_in)
    snof = [dv(V.tensor_scalar(T.snof[:, 48 * t:48 * t + 48], T.snw[:, :], 4, 16 + t, A.mult, A.add)) for t in range(4)]
    turn = CAP * (N - 1 - r)

    def pick_x(who, lo, hi):
        marks = []
        for t in sorted(range(4), key=lambda t: (who[:t].count(who[t]), t)):
            for a, b in ((lo, min(hi, turn)), (max(lo, turn), hi)):
                if a < b and who[t] != ".":
                    e = 48 * t + (a + CAP * (r + 1)) % ALL // 16
                    marks.append(move(who[t], T.xt[:, 4 * (32 + a) + t:4 * (32 + b):4],
                                      T.xb[:, 0:528].indirect(T.snof[:, e:e + (b - a) // 16]), x_in, m_pad, snof[t]))
        return marks

    def quantise(codes, planes, at, tile, lo, hi, marks):
        need("V", *marks)
        return dv(V.quantize_mx(codes[:, at:at + hi - lo], planes[:, at:at + hi - lo], tile[:, 4 * lo:4 * hi]))

    below, above = (32, 0) if turn == CAP else (0, 32)
    f_q = []
    for i, (steps, over, calls) in enumerate(PLAN["f"]):
        lo, hi = CAP * (7 - steps[-1]), CAP * (8 - steps[0])
        if i == 0:
            lo, hi = lo - below, hi + above
        low = lo + (above if lo == CAP else 0)
        if over:
            marks = pick_x("SS.V", low, hi) + pick_x("..V.", low, hi - over) + pick_x("..S.", hi - over, hi)
        else:
            marks = pick_x("SSVV", low, hi)
        f_q = [quantise(T.cf, T.sf, 32 + lo, T.xt, 32 + lo, 32 + hi, marks + (f_q if lo == CAP else []))]
        need("G", *f_q)
        send("f", calls)
    own = pick_x("SSSS", 7 * CAP, ALL)

    need("V", n8_in, m_pi)
    p_a = dv(V.tensor_scalar(T.pa[:, :], T.nb8[:, :], 15, None, A.bitwise_and))
    p_b = dv(V.tensor_scalar(T.pb[:, :], T.nb8[:, :], 4, None, A.arith_shift_right))
    k12 = dv(V.tensor_scalar(T.k12[:, :], T.pi[:, :], 12, None, A.bitwise_and))
    need("V", p_a)
    p_c = dv(V.tensor_scalar(T.pc[:, :], T.pa[:, :], 48, None, A.mult))
    need("V", m_iv)
    m_ivv = dv(V.tensor_tensor(T.ivv[:, :], T.iv1[:, :], T.iv2[:, :], A.add))
    need("V", p_c, p_b)
    p_d = dv(V.tensor_tensor(T.pd[:, :], T.pc[:, :], T.pb[:, :], A.add))
    k3 = dv(V.tensor_scalar(T.k3[:, :], T.pi[:, :], 3, None, A.bitwise_and))
    need("V", p_d)
    p_of = dv(V.tensor_copy(T.pof[:, :], T.pd[:, :]))
    need("V", k12)
    m_f12 = dv(V.tensor_copy(T.f12[:, :], T.k12[:, :]))
    need("V", p_of, m_inv, m_ivv)
    m_sc = dv(V.tensor_copy(T.inv[:, 0:ALL].indirect(T.pof[:, 0:8]), T.ivv[:, :]))
    need("V", w_in)
    w_q = dv(V.quantize_mx(T.wq[:, 0:512], T.ws[:, 0:512], T.wb[:, 0:2048]))
    own_f = quantise(T.cf, T.sf, 32 + 7 * CAP, T.xt, 32 + ALL - 128, 32 + ALL, own + f_q)
    need("V", m_f12, k3)
    m_fgr = dv(V.tensor_scalar(T.fgr[:, :], T.k3[:, :], 128, T.f12[:, :], A.mult, A.add))
    need("V", nb_in)
    for bl in range(2):
        m_zo = dv(V.tensor_scalar(T.zof[:, bl:64:2], T.nbw[:, :], ALL * bl, None, A.add))
    need("V", m_fgr, m_grp)
    m_gro = dv(V.tensor_scalar(T.gro[:, :], T.grpat[:, :], T.fgr[:, :], None, A.add))
    m_d0 = dv(V.memset(T.d0[:, 0:2048:4], 0.0))

    def lay_gr(p, *marks):
        return move("S", T.d1[:, 0:1024:4], T.grb[:, 0:512].indirect(T.gro[:, 16 * p:16 * p + 16]), m_gro, gr_in, *marks)

    need("G", m_sc)
    done(g.dma_start(T.inv[0:1, :], T.inv[32:33, :], accum_op=A.add), "d_add", 16)
    added = done(g.dma_start(T.inv[16:17, :], T.inv[48:49, :], accum_op=A.add), "d_add", 16)
    m_ca = iota(T.ca[:, :], [[0, 512], [-1, 2]])
    for b in range(4):
        m_up = iota(T.ub[:, UW * b:UW * b + 8], [[0, 8]])
    m_fip = dg(g.iota(T.fipat[:, :], [[4, 2], [1, 4], [128, 2]], 0, 0))
    m_c1 = iota(T.cs8[:, :], [[0, 1024]], 1)
    need("G", m_c1)
    m_cs = iota(T.cs8[:, 0:1024:8], [[0, 128]])

    need("Y", added)
    for k in range(8):
        for e in range(2):
            iv_in = done(Y.dma_start(T.invw[16 * k:16 * k + 16, 48 * e:48 * e + 48], T.inv[16 * e:16 * e + 1, :]), "d_iv", 16)
    for s in range(4):
        done(Y.dma_start(T.ild[:, 16 * s:16 * s + 16], T.il[s:16:4, :]), "d_id", 16)
    id_in = done(Y.dma_start(T.ild[:, 64:128], T.il[:, :]), "d_id", 16)
    need("Y", arrived["f"][-1])
    v_in = done(Y.dma_start(T.vb[:, :], T.w2[:, :]), "d_v", 16)
    need("Y", id_in)
    for k in range(8):
        il_in = done(Y.dma_start(T.ilw[16 * k:16 * k + 16, :], T.ild[:, :]), "d_il", 16)

    zp_free = {}

    def products(ph, grp, st, sts, land, wide, pad, *ready):
        steps, bank = GROUPS[ph][grp], len(zp_free.setdefault("turns", [])) % 2
        zp_free["turns"].append(grp)
        n = len(steps)
        if ph == "f":
            lo, first = 32 + 7 * CAP + 32 + CAP * steps[0], r + steps[0]
        else:
            lo, first = CAP * (7 - steps[-1]), r - steps[-1]
        need("P", arrived[ph][grp], *ready)
        mm = []
        for b in range(4):
            at = 512 * (2 * b + bank)
            need("P", *zp_free.get((b, bank), []))
            mm.append(done(P.matmul_mx(T.zp[:, at:at + CAP * n], st[:, 128 * b:128 * b + 128], sts[:, 128 * b:128 * b + 128],
                                       T["c" + ph][:, lo:lo + CAP * n], T["s" + ph][:, lo:lo + CAP * n], True, True), "ct"))

        def take(q, b):
            at, to = 512 * (2 * b + bank), wide * b + pad
            zp_free[(b, bank)] = [move(q, land[:, to + CAP * d:to + CAP * (d + k)], T.zp[:, at + CAP * o:at + CAP * (o + k)],
                                       mm[b]) for o, d, k in runs(first, n)]
            return zp_free[(b, bank)]
        return take

    zb_ok = {b: [] for b in range(4)}
    for grp in range(len(GROUPS["f"])):
        take = products("f", grp, T.wq, T.ws, T.zb, ALL, 0, w_q, own_f)
        if grp < len(GROUPS["f"]) - 1:
            for q, b in zip("SVSV", range(4)):
                zb_ok[b] += take(q, b)
    zb_ok[0] += take("S", 0)
    zb_ok[1] += take("V", 1)

    def zpick(p, k, lo=0, hi=16):
        return T.zb[:, 2 * ALL * p:2 * ALL * (p + 1)].indirect(T.zof[:, 16 * k + lo:16 * k + hi])

    def seg(name, p):
        return T[name][:, 256 * p:256 * p + 256]

    c = {}
    c["z0", 0] = [move("S", T.z0[:, 0:128], zpick(0, 0, 0, 8), m_zo, *zb_ok[0], *zb_ok[1]),
                  move("V", T.z0[:, 128:256], zpick(0, 0, 8, 16), m_zo, *zb_ok[0], *zb_ok[1])]
    zb_ok[2] += take("S", 2)
    zb_ok[3] += take("S", 3)
    d1_ok = {0: lay_gr(0, m_d1)}
    c["z0", 1] = [move("S", seg("z0", 1), zpick(1, 0), *zb_ok[2], *zb_ok[3])]

    def vmax(p, k):
        src, dst = (("z0", "m1"), ("m1", "m2"))[k - 1]
        need("V", *c[src, p])
        c[dst, p] = [dv(V.tensor_tensor(seg(dst, p), zpick(p, k), seg(src, p), A.max))]

    def vrec(p, k):
        src = ("z0", "m1", "m2")[k - 1]
        need("V", *c[src, p])
        c["n", p, k] = dv(V.tensor_tensor(T.d0[:, 1024 * p + 4 - k:1024 * p + 1024:4], zpick(p, k), seg(src, p), A.is_le))

    def keep(p):
        need("V", m_d0, d1_ok[p], *[c["n", p, k] for k in (1, 2, 3)])
        c["k", p] = dv(V.tensor_tensor_scan(T.gg[:, 2048 * p:2048 * p + 1024], T.d0[:, 1024 * p:1024 * p + 1024],
                                            T.d1[:, :], 0.0, A.mult, A.add))

    def odd(p):
        need("V", m_ca, c["k", p])
        c["a", p] = dv(V.tensor_tensor_scan(T.gg[:, 2048 * p + 1024:2048 * p + 2048], T.ca[:, :],
                                            T.gg[:, 2048 * p:2048 * p + 1024], 0.0, A.mult, A.subtract))

    def second(p):
        need("V", c["a", p])
        k2 = T.gg[:, 2048 * p + 1:2048 * p + 1024:4]
        c["g", p] = dv(V.tensor_tensor(k2, k2, T.gg[:, 2048 * p + 2:2048 * p + 1024:4], A.subtract))

    def place(q, b, lo, hi):
        p, bl = divmod(b, 2)
        return move(q, T.h[:, 4 * lo + b:4 * hi:4],
                    T.gg[:, 2048 * p + 64 * bl:2048 * p + 2048].indirect(T.ivo[:, lo // 16:hi // 16]), c["g", p], *iv_ok)

    vmax(0, 1); vrec(0, 1); vmax(0, 2); vrec(0, 2); vrec(0, 3)
    vmax(1, 1); keep(0); vrec(1, 1); odd(0)
    d1_ok[1] = lay_gr(1, c["k", 0])
    need("V", iv_in)
    iv_sum = dv(V.tensor_tensor(T.invs[:, :], T.invw[:, 0:48], T.invw[:, 48:96], A.add))
    second(0)
    need("V", iv_sum)
    iv_ok = [dv(V.tensor_copy(T.ivo[:, 6 * o:6 * (o + k)], T.invs[:, 6 * d:6 * (d + k)])) for o, d, k in runs(r, N)]
    h_ok = [place("S", 0, 0, ALL), place("S", 1, 0, ALL)]
    vmax(1, 2); vrec(1, 2); vrec(1, 3); keep(1); odd(1); second(1)
    spare = max(0, 128 - CAP * len(PLAN["b"][0][0]))
    for i, (steps, over, calls) in enumerate(PLAN["b"]):
        lo, hi = CAP * steps[0] - (spare if i == 0 else 0), CAP * (steps[-1] + 1)
        marks = [place("S", 2, lo, hi), place("V", 3, lo, hi - over)] + ([place("S", 3, hi - over, hi)] if over else [])
        b_q = quantise(T.cb, T.sb, 7 * CAP + 32 + lo, T.h, lo, hi, marks + h_ok)
        need("G", b_q)
        send("b", calls)
    own = [place("S", 2, 0, CAP - spare), place("S", 3, 0, CAP - spare)]

    need("V", v_in)
    v_q = dv(V.quantize_mx(T.vq[:, 0:512], T.vs[:, 0:512], T.vb[:, 0:2048]))
    own_b = quantise(T.cb, T.sb, 7 * CAP, T.h, 0, 128, own + [b_q])
    k15 = dv(V.tensor_scalar(T.k15[:, :], T.pi[:, :], 15, None, A.bitwise_and))
    need("V", il_in)
    m_iq = dv(V.tensor_scalar(T.ilq[:, :], T.ilw[:, :], 8, None, A.add))
    need("V", k15)
    m_f8 = dv(V.tensor_scalar(T.f8[:, :], T.k15[:, :], 8, None, A.mult))
    need("V", m_f8, m_fip)
    m_fio = dv(V.tensor_scalar(T.fio[:, :], T.fipat[:, :], T.f8[:, :], None, A.add))

    ub_ok = {b: [m_iq, m_up] for b in range(4)}
    for grp in range(len(GROUPS["b"])):
        take = products("b", grp, T.vq, T.vs, T.ub, UW, 8, v_q, own_b)
        if grp < len(GROUPS["b"]) - 1:
            for q, b in zip("SVSV", range(4)):
                ub_ok[b] += take(q, b)

    def upick(b, lo, hi):
        return T.ub[:, UW * b:UW * b + UW].indirect(T.ilq[:, lo:hi])

    def part(name, b, s, n=256):
        return T[name][:, 1024 * b + n * s:1024 * b + n * (s + 1)]

    a = {}

    def copy(q, b):
        ub_ok[b] += take(q, b)

    def first(q, b):
        a[b] = move(q, part("acc", b, 0), upick(b, 0, 16), *ub_ok[b])

    def chain(b, s):
        need("V", a[b], *ub_ok[b])
        a[b] = dv(V.tensor_tensor(part("acc", b, s), upick(b, 16 * s, 16 * s + 16), part("acc", b, s - 1), A.add))

    def half(q, b):
        a["h", b] = move(q, T.fin[:, 128 * b:128 * b + 128], part("acc", b, 3).indirect(T.fio[:, 0:8]), a[b], m_fio)

    def close(b):
        need("V", a["h", b], a[b], m_fio)
        a["y", b] = dv(V.tensor_tensor(T.yb[:, 128 * b:128 * b + 128], part("acc", b, 3).indirect(T.fio[:, 8:16]),
                                       T.fin[:, 128 * b:128 * b + 128], A.add))

    def spread(q, b, s, n):
        a["s", b, s] = move(q, part("acc", b, s, 1024 // n), upick(b, 64 + 64 // n * s, 64 + 64 // n * (s + 1)), *ub_ok[b])

    def scan(b, s, n):
        need("V", a["s", b, s], m_cs)
        a["t", b, s] = dv(V.tensor_tensor_scan(part("sum", b, s, 1024 // n), T.cs8[:, 0:1024 // n],
                                               part("acc", b, s, 1024 // n), 0.0, A.mult, A.add))

    def ends(q, b, n):
        a["y", b] = move(q, T.yb[:, 128 * b:128 * b + 128], T.sum[:, 1024 * b + 7:1024 * b + 1024:8],
                         *[a["t", b, s] for s in range(n)])

    def store(lo, hi):
        need("Y", *[a["y", b] for b in range(lo, hi)])
        return done(Y.dma_start(T.y[:, 128 * lo:128 * hi], T.yb[:, 128 * lo:128 * hi]), "d_y", 16)

    copy("S", 0); copy("V", 1); first("S", 0); first("V", 1)
    copy("S", 2); spread("S", 2, 0, 1)
    for s in (1, 2, 3):
        chain(0, s); chain(1, s)
    copy("S", 3); spread("S", 3, 0, 2); half("S", 0); half("S", 1); spread("S", 3, 1, 2)
    scan(2, 0, 1); close(0); close(1); store(0, 2)
    scan(3, 0, 2); ends("S", 2, 1); store(2, 3); scan(3, 1, 2); ends("V", 3, 2)
    y_out = store(3, 4)
    need("Y", y_out)
    need("G", ("ls", cnt["ls"]))
